import numpy as np
import ml_dtypes


def mxq(x, axis, fmt="e4m3"):
    dtype, down = {"e4m3": (ml_dtypes.float8_e4m3fn, 7), "e5m2": (ml_dtypes.float8_e5m2, 14)}[fmt]
    v = np.moveaxis(np.asarray(x, np.float32).astype(ml_dtypes.bfloat16).astype(np.float64), axis, -1)
    blocks = v.reshape(v.shape[:-1] + (-1, 32))
    amax = np.abs(blocks).max(-1, keepdims=True)
    byte = np.maximum(np.where(amax > 0, np.frexp(amax)[1] - 1 + 127, 0) - down, 1)
    scale = np.exp2(byte - 127.0)
    codes = (blocks / scale).astype(np.float32).astype(dtype).astype(np.float64)
    return np.moveaxis((codes * scale).reshape(v.shape), -1, axis)


WIDE = False


def mx_kscale(k):
    if not WIDE:
        return np.ones(k)
    levels = np.array([10, -10, 5, -5, 0])
    if k % 512:
        return np.exp2(np.random.permutation(np.resize(levels, k // 32))).repeat(32)
    a = np.empty((k // 512, 16))
    for p in range(k // 512):
        a[p, :8] = np.random.permutation(np.resize(levels, 8))
        for g in range(8):
            far = levels[np.abs(levels - a[p, g]) >= 10]
            a[p, g + 8] = far[np.random.randint(len(far))]
    return np.exp2(a.ravel()).repeat(32)


BF16 = ml_dtypes.bfloat16


def bf(x):
    return np.asarray(x, np.float32).astype(BF16)


def f64(x):
    return np.asarray(x).astype(np.float64)


E2M1 = np.array([0.0, 0.5, 1.0, 1.5, 2.0, 3.0, 4.0, 6.0, -0.0, -0.5, -1.0, -1.5, -2.0, -3.0, -4.0, -6.0])


def pack_weight(w, fmt):
    k, n = w.shape
    w = f64(bf(w)).reshape(k // 32, 32, n)
    amax = np.abs(w).max(1)
    if fmt == "e4m3":
        byte = np.frexp(amax)[1] - 1 + 127 - 7
    else:
        mant, ex = np.frexp(amax / 6.0)
        byte = np.where(mant > 0.5, ex, ex - 1) + 127
    byte = np.clip(np.where(amax > 0, byte, 1), 1, 254)
    scaled = (w * np.exp2(127.0 - byte)[:, None, :]).reshape(k, n).astype(np.float32)
    by_word = np.ascontiguousarray(scaled.reshape(k // 512, 128, 4, n).transpose(0, 1, 3, 2))
    if fmt == "e4m3":
        words = by_word.astype(ml_dtypes.float8_e4m3fn).view(np.uint8)
    else:
        c = by_word.astype(ml_dtypes.float4_e2m1fn).view(np.uint8) & 0xF
        words = c[..., 0::2] | (c[..., 1::2] << 4)
    return np.ascontiguousarray(words), np.ascontiguousarray(byte.astype(np.uint8).reshape(k // 512, 16, n))


def unpack_weight(words, scales, fmt):
    g, p, n, _ = words.shape
    if fmt == "e4m3":
        vals = np.ascontiguousarray(words).view(ml_dtypes.float8_e4m3fn).astype(np.float64)
    else:
        nib = np.empty((g, p, n, 4), np.uint8)
        nib[..., 0::2] = words & 0xF
        nib[..., 1::2] = words >> 4
        vals = E2M1[nib]
    vals = vals * np.repeat(np.exp2(scales.astype(np.float64) - 127.0), 8, axis=1)[..., None]
    return vals.transpose(0, 1, 3, 2).reshape(g * 512, n)
def pack4(w):
    words, scales = pack_weight(w, "e2m1")
    return words.reshape(words.shape[0], 128, -1), scales


def unpack4(words, scales):
    return unpack_weight(words.reshape(words.shape[0], 128, -1, 2), scales, "e2m1")


def planes(Y):
    n, m = Y.shape
    b = f64(bf(Y)).reshape(n // 32, 32, m)
    amax = np.abs(b).max(1)
    byte = np.clip(np.where(amax > 0, np.frexp(amax)[1] - 1 + 127 - 7, 1), 1, 254)
    codes = (b * np.exp2(127.0 - byte)[:, None, :]).reshape(n, m).astype(np.float32).astype(ml_dtypes.float8_e4m3fn).view(np.uint8)
    words = codes.reshape(n // 512, 128, 4, m).transpose(0, 1, 3, 2)
    return np.ascontiguousarray(words), np.ascontiguousarray(byte.astype(np.uint8).reshape(n // 512, 16, m))


N, L = 1024, 1024
EPS = 0.3
FLOOR = 0.02

def soft_box(lo, hi):
    half = np.random.uniform(lo, hi, (N, 1))
    d = np.abs(np.arange(N)[:, None] - np.arange(N)[None, :])
    d = np.minimum(d, N - d)
    return np.where(d <= half, 1.0, FLOOR) * np.exp(0.3 * np.random.randn(N, N))

def setup_inputs():
    s, t = mx_kscale(N), mx_kscale(N)
    win = soft_box(N // 64, N // 32)
    win = win / win.sum(axis=1, keepdims=True)
    blend = soft_box(N // 512, N // 128)
    conf = np.exp(0.5 * np.random.randn(N))
    norm = 1.0 / (win @ (blend @ conf))
    spread = np.exp(0.8 * np.random.randn(L))
    guide = np.random.randn(N, L)
    image = spread * (0.5 * np.random.randn(L) * guide + 2.0 * np.random.randn(N, L))
    base = 0.5 * spread * np.random.randn(N, L)
    win_words, win_scales = pack4(win.T * s[:, None])
    cross_words, cross_scales = pack_weight(guide * image / s[:, None], "e4m3")
    return {"win_words": win_words, "win_scales": win_scales,
            "cross_words": cross_words, "cross_scales": cross_scales,
            "square": bf((guide * guide + EPS) / s[:, None]),
            "blend": bf(blend * t[None, :] / s[:, None]),
            "conf": bf(conf / t), "norm": bf(norm), "guide": bf(guide), "base": bf(base)}

def reference(win_words, win_scales, cross_words, cross_scales, square, blend, conf, norm, guide, base):
    V = unpack4(win_words, win_scales)
    C = unpack_weight(cross_words, cross_scales, "e4m3")
    num = V.T @ C
    den = V.T @ mxq(f64(square), 0, "e4m3")
    T = V.T @ mxq(f64(blend), 0, "e4m3")
    A = f64(conf)[:, None] * num / den
    mean_a = mxq(T, 1, "e4m3") @ mxq(A, 0, "e4m3")
    y = mean_a * f64(norm)[:, None] * f64(guide) + f64(base)
    words, scales = planes(y.T)
    return y, words, scales

@@ -1,0 +1,432 @@
+from contextlib import ExitStack
+
+import concourse.mybir as mybir
+from concourse.masks import make_identity
+
+N, L = 1024, 1024
+FLOPS = 4 * 2 * N * N * L
+
+F32 = mybir.dt.float32
+BF16 = mybir.dt.bfloat16
+I32 = mybir.dt.int32
+U32 = mybir.dt.uint32
+U8 = mybir.dt.uint8
+FP8X4 = mybir.dt.float8_e4m3fn_x4
+FP4X4 = mybir.dt.float4_e2m1fn_x4
+ACT = mybir.ActivationFunctionType
+ALU = mybir.AluOpType
+
+P = 128
+PACK = 4
+PASS = P * PACK
+GROUPS = N // PASS
+TILES = N // P
+PIECE = 128
+SCALAR_PIECES = (3, 3, 2)
+HEAD_SCALAR = 192
+LAST_SCALAR = 128
+T0_ENG = ("scalar", "scalar")
+T_FIRST = 11
+LAG = 2
+BL_FIRST = 1
+BL_STEP = 3
+WORD_TILES = 2
+
+
+def tile_mean_free_guided_pass_k4_kernel(
+    tc, win_words, win_scales, cross_words, cross_scales, square, blend, conf, norm, guide, base,
+    out_0, out_1, out_2,
+):
+    nc = tc.nc
+    with ExitStack() as ctx:
+        keep = ctx.enter_context(tc.tile_pool(name="keep", bufs=1))
+        work = ctx.enter_context(tc.tile_pool(name="work", bufs=2))
+        psum = ctx.enter_context(tc.psum_pool(name="psum", bufs=8))
+        ctx.enter_context(tc.manual_schedule())
+
+        def kept(name, shape, dtype):
+            return keep.tile(shape, dtype, name=name, align_bytes=64)
+
+        def rotating(tag, shape, dtype, bufs):
+            return work.tile(shape, dtype, name=tag, tag=tag, bufs=bufs, align_bytes=64)
+
+        def bank():
+            return psum.tile([P, PASS], F32, name="bank", tag="bank")
+
+        v_words = [kept("v_words%d" % h, [P, GROUPS, N], U8) for h in range(2)]
+        v_scales = kept("v_scales", [P, GROUPS, N], U8)
+        vp_words = [kept("vp_words%d" % h, [P, GROUPS, N], U8) for h in range(2)]
+        vp_scales = kept("vp_scales", [P, GROUPS, N], U8)
+        c_scales = kept("c_scales", [P, GROUPS, L], U8)
+        c_words = [kept("c_words%d" % lh, [P, GROUPS, PASS], U32) for lh in range(2)]
+        sq_raw = {(g, lh): kept("sq_raw%d%d" % (g, lh), [P, PACK, PASS], BF16) for g in range(2) for lh in range(2)}
+        bl_raw = {(g, h): kept("bl_raw%d%d" % (g, h), [P, PACK, PASS], BF16) for g in range(2) for h in range(2)}
+        gd = [kept("guide%d" % i, [P, 2, L], BF16) for i in range(TILES // 2)]
+        bs = [kept("base%d" % i, [P, 2, L], BF16) for i in range(TILES // 2)]
+        pairs = [(a, b) for a in range(2) for b in range(2)]
+        sq_q = {k: (kept("sq_c%d%d" % k, [P, PASS], U32), kept("sq_s%d%d" % k, [P, PASS], U8)) for k in pairs}
+        bl_q = {k: (kept("bl_c%d%d" % k, [P, PASS], U32), kept("bl_s%d%d" % k, [P, PASS], U8)) for k in pairs}
+        a_q = {k: (kept("a_c%d%d" % k, [P, PASS], U32), kept("a_s%d%d" % k, [P, PASS], U8)) for k in pairs}
+        t_q = [(kept("t_c%d" % j, [P, 2 * P], U32), kept("t_s%d" % j, [P, 2 * P], U8)) for j in range(TILES)]
+        y_words = {
+            (lh, i): kept("y_words%d%d" % (lh, i), [P, WORD_TILES * P], U32)
+            for lh in range(2) for i in range(TILES // WORD_TILES)
+        }
+        y_scales = kept("y_scales", [P, 2, N], U8)
+        rows = kept("rows", [P, 3 * P], BF16)
+        ident = kept("ident", [P, P], F32)
+        ident_bf = kept("ident_bf", [P, TILES], BF16)
+        cols = kept("cols", [P, 2 * TILES], F32)
+
+        warm = kept("warm", [P, 2], F32)
+
+        nc.vector.memset(v_scales[:].rearrange("p g n -> p (g n)").bitcast(I32), 0)
+        nc.vector.memset(c_scales[:].rearrange("p g n -> p (g n)").bitcast(I32), 0)
+
+        def load_scales(plane, dram):
+            for q in range(4):
+                nc.sync.dma_start(
+                    out=plane[32 * q : 32 * q + 4].bitcast(I32),
+                    in_=dram[:, 4 * q : 4 * q + 4, :].rearrange("g r n -> r g n").bitcast(I32),
+                )
+
+        def load_rows(raw, dram, g, half):
+            nc.sync.dma_start(
+                out=raw[g, half][:],
+                in_=dram[PASS * g : PASS * (g + 1), PASS * half : PASS * (half + 1)].rearrange("(p j) l -> p j l", j=PACK),
+            )
+
+        def load_cross(lh):
+            nc.sync.dma_start(
+                out=c_words[lh][:].bitcast(I32),
+                in_=cross_words.rearrange("g p l t -> p g (l t)")[:, :, PACK * PASS * lh : PACK * PASS * (lh + 1)].bitcast(I32),
+            )
+
+        def load_window(h):
+            nc.sync.dma_start(
+                out=v_words[h][:].bitcast(I32),
+                in_=win_words.rearrange("g p b -> p g b")[:, :, N * h : N * (h + 1)].bitcast(I32),
+            )
+
+        load_window(0)
+        load_rows(sq_raw, square, 0, 0)
+        load_scales(v_scales, win_scales)
+        load_rows(sq_raw, square, 1, 0)
+        load_rows(sq_raw, square, 0, 1)
+        load_scales(c_scales, cross_scales)
+        load_rows(sq_raw, square, 1, 1)
+        load_cross(0)
+        load_window(1)
+        load_rows(bl_raw, blend, 1, 0)
+        load_rows(bl_raw, blend, 0, 0)
+        load_rows(bl_raw, blend, 1, 1)
+        load_rows(bl_raw, blend, 0, 1)
+        load_cross(1)
+        for i in range(TILES // 2):
+            for dst, src in ((gd, guide), (bs, base)):
+                nc.sync.dma_start(
+                    out=dst[i][:], in_=src[2 * P * i : 2 * P * (i + 1), :].rearrange("(j p) l -> p j l", p=P)
+                )
+
+        nc.gpsimd.memset(rows[:], 0.0)
+        nc.gpsimd.dma_start(
+            out=rows[0:PACK, 0 : 2 * P].rearrange("t (m r) -> t m r", r=4),
+            in_=conf.rearrange("(m t r) -> t m r", t=PACK, r=4),
+        )
+        nc.gpsimd.dma_start(out=rows[0:TILES, 2 * P : 3 * P], in_=norm.rearrange("(j p) -> j p", p=P))
+        make_identity(nc, ident[:])
+        nc.gpsimd.tensor_copy(out=ident_bf[:], in_=ident[:, 0:TILES])
+
+        def copy_on(engine, out, in_):
+            if engine == "scalar":
+                nc.scalar.copy(out=out, in_=in_)
+            else:
+                nc.vector.tensor_copy(out=out, in_=in_)
+
+        def quantize(dst_codes, dst_scales, src):
+            nc.vector.quantize_mx(out=dst_codes.bitcast(FP8X4), scales=dst_scales, in_=src)
+
+        def weave_rows(engine, woven, raw, c0, c1):
+            copy_on(
+                engine,
+                woven[:, PACK * c0 : PACK * c1].rearrange("p (c i j) -> p c j i", i=4, j=PACK),
+                raw[:, :, c0:c1].rearrange("p j (c i) -> p c j i", i=4),
+            )
+
+        def weave_blend(engine, woven, raw, c0, c1):
+            slots_here = slice(c0 // P, c1 // P)
+            copy_on(
+                engine,
+                woven[:].rearrange("p (t m r j) -> p m t j r", t=PACK, r=4, j=PACK)[:, :, slots_here],
+                raw[:].rearrange("p j (m t r) -> p m t j r", t=PACK, r=4)[:, :, slots_here],
+            )
+
+        def new_woven():
+            return rotating("woven", [P, PACK * PASS], BF16, 5)
+
+        nc.vector.memset(warm[:, 0:1], 1.0)
+        nc.scalar.activation(out=warm[:, 1:2], in_=warm[:, 0:1], func=ACT.Abs_reciprocal_sqrt)
+        head = [new_woven(), new_woven()]
+        def sort_window(h):
+            nc.vector.tensor_copy(
+                out=vp_words[h][:].bitcast(I32).rearrange("p g (t m w) -> p g t m w", t=PACK, w=2),
+                in_=v_words[h][:].bitcast(I32).rearrange("p g (m t w) -> p g t m w", t=PACK, w=2),
+            )
+
+        sort_window(0)
+        weave_rows("scalar", head[0], sq_raw[0, 0], 0, HEAD_SCALAR)
+        weave_rows("vector", head[0], sq_raw[0, 0], HEAD_SCALAR, PASS)
+        nc.vector.tensor_copy(
+            out=vp_scales[:].bitcast(I32).rearrange("p g (h t m) -> p (g h) t m", h=2, t=PACK),
+            in_=v_scales[:].bitcast(I32).rearrange("p g (h m t) -> p (g h) t m", h=2, t=PACK),
+        )
+        quantize(sq_q[0, 0][0][:], sq_q[0, 0][1][:], head[0][:])
+        weave_rows("scalar", head[1], sq_raw[1, 0], 0, HEAD_SCALAR)
+        weave_rows("vector", head[1], sq_raw[1, 0], HEAD_SCALAR, PASS)
+        col_bank = bank()
+        for h in range(2):
+            nc.tensor.matmul(
+                col_bank[:, PACK * h : PACK * (h + 1)], lhsT=rows[:, P * h : P * (h + 1)], rhs=ident_bf[:, 0:PACK],
+                start=True, stop=True,
+            )
+        nc.tensor.matmul(
+            col_bank[:, TILES : 2 * TILES], lhsT=rows[:, 2 * P : 3 * P], rhs=ident_bf[:], start=True, stop=True
+        )
+        quantize(sq_q[1, 0][0][:], sq_q[1, 0][1][:], head[1][:])
+        nc.scalar.copy(out=cols[:], in_=col_bank[:, 0 : 2 * TILES])
+
+        def moment(s, operand):
+            (h, lh), t = units[slots[s][0]], slots[s][1]
+            slot = PACK * h + t
+            acc = bank()
+            for g in range(GROUPS):
+                codes, scales = operand(g, lh)
+                nc.tensor.matmul_mx(
+                    out=acc[:],
+                    lhsT=vp_words[h][:, g, 2 * P * t : 2 * P * (t + 1)].bitcast(FP4X4),
+                    lhsT_scale=vp_scales[:, g, P * slot : P * (slot + 1)],
+                    rhs=codes.bitcast(FP8X4), rhs_scale=scales,
+                    start=(g == 0), stop=(g == GROUPS - 1),
+                )
+            return acc
+
+        def square_operand(g, lh):
+            return sq_q[g, lh][0][:], sq_q[g, lh][1][:]
+
+        def cross_operand(g, lh):
+            return c_words[lh][:, g, :], c_scales[:, g, PASS * lh : PASS * (lh + 1)]
+
+        def t_matmuls(j):
+            banks = [bank(), bank()]
+            for h in range(2):
+                for t in range(PACK):
+                    for g in range(GROUPS):
+                        nc.tensor.matmul_mx(
+                            out=banks[h][:, P * t : P * (t + 1)],
+                            lhsT=bl_q[g, h][0][:, P * t : P * (t + 1)].bitcast(FP8X4),
+                            lhsT_scale=bl_q[g, h][1][:, P * t : P * (t + 1)],
+                            rhs=v_words[j // PACK][:, g, 2 * P * (j % PACK) : 2 * P * (j % PACK + 1)].bitcast(FP4X4),
+                            rhs_scale=v_scales[:, g, P * j : P * (j + 1)],
+                            start=(g == 0), stop=(g == GROUPS - 1),
+                        )
+            return banks
+
+        def t_copy(banks, engines=("scalar", "scalar")):
+            woven = rotating("t_woven", [P, 2 * PASS], BF16, 2)
+            for h in range(2):
+                copy_on(
+                    engines[h],
+                    woven[:, PASS * h : PASS * (h + 1)].rearrange("p (n t) -> p n t", t=PACK),
+                    banks[h][:].rearrange("p (t n) -> p n t", t=PACK),
+                )
+            return woven
+
+        def t_quantize(j, woven):
+            quantize(t_q[j][0][:], t_q[j][1][:], woven[:])
+
+        def mean_matmuls(j, lh):
+            acc = bank()
+            for h in range(2):
+                nc.tensor.matmul_mx(
+                    out=acc[:],
+                    lhsT=t_q[j][0][:, P * h : P * (h + 1)].bitcast(FP8X4),
+                    lhsT_scale=t_q[j][1][:, P * h : P * (h + 1)],
+                    rhs=a_q[h, lh][0][:].bitcast(FP8X4), rhs_scale=a_q[h, lh][1][:],
+                    start=(h == 0), stop=(h == 1),
+                )
+            return acc
+
+        units = [(h, lh) for lh in range(2) for h in range(2)]
+        slots = [(u, t) for u in range(len(units)) for t in range(PACK)]
+        later = [
+            (lambda e, w, g, c0, c1: weave_rows(e, w, sq_raw[g, 1], c0, c1), lambda g: sq_q[g, 1]),
+            (lambda e, w, g, c0, c1: weave_blend(e, w, bl_raw[g, 0], c0, c1), lambda g: bl_q[g, 0]),
+            (lambda e, w, g, c0, c1: weave_blend(e, w, bl_raw[g, 1], c0, c1), lambda g: bl_q[g, 1]),
+        ]
+        root, recip, nums, a_rows, a_woven, prep, t_banks, t_woven = {}, {}, {}, {}, {}, {}, {}, {}
+
+        def square_root_step(s):
+            recip[s] = rotating("recip", [P, PASS], F32, 4)
+            nc.scalar.activation(out=recip[s][:], in_=root[s][:], func=ACT.Square)
+
+        def ratio(s):
+            u, t = slots[s]
+            if t == 0:
+                a_rows[u] = rotating("a_rows", [P, PACK, PASS], BF16, 2)
+            slot = PACK * units[u][0] + t
+            nc.vector.scalar_tensor_tensor(
+                out=a_rows[u][:, t, :], in0=nums[s][:], scalar=cols[:, slot : slot + 1], in1=recip[s][:],
+                op0=ALU.mult, op1=ALU.mult,
+            )
+
+        def a_weave(u, scalar_columns=0):
+            a_woven[u] = rotating("a_woven", [P, PACK * PASS], BF16, 2)
+            if scalar_columns:
+                weave_rows("scalar", a_woven[u], a_rows[u], 0, scalar_columns)
+            weave_rows("vector", a_woven[u], a_rows[u], scalar_columns, PASS)
+
+        def a_quantize(u):
+            quantize(a_q[units[u]][0][:], a_q[units[u]][1][:], a_woven[u][:])
+
+        def prep_quantize(u, g):
+            codes, scales = later[u][1](g)
+            quantize(codes[:], scales[:], prep[u, g][:])
+
+        prep[0, 0], prep[0, 1] = new_woven(), new_woven()
+        later[0][0]("scalar", prep[0, 0], 0, 0, PIECE * SCALAR_PIECES[0])
+        means = {}
+        for s in range(len(slots) + LAG):
+            if s < len(slots):
+                den = moment(s, square_operand)
+                root[s] = rotating("root", [P, PASS], F32, 2)
+                nc.scalar.activation(out=root[s][:], in_=den[:], func=ACT.Abs_reciprocal_sqrt)
+            if 0 < s <= len(slots):
+                nums[s - 1] = moment(s - 1, cross_operand)
+                square_root_step(s - 1)
+            if s >= LAG:
+                ratio(s - LAG)
+            if s == 0:
+                later[0][0]("vector", prep[0, 0], 0, PIECE * SCALAR_PIECES[0], PASS)
+                later[0][0]("vector", prep[0, 1], 1, 0, PASS)
+                prep_quantize(0, 0)
+                sort_window(1)
+                prep_quantize(0, 1)
+            for b in (1, 2):
+                at = s - (BL_FIRST + BL_STEP * (b - 1))
+                if at == 0:
+                    prep[b, 0], prep[b, 1] = new_woven(), new_woven()
+                    later[b][0]("vector", prep[b, 1], 1, 0, PASS)
+                if at == 1:
+                    later[b][0]("vector", prep[b, 0], 0, PIECE * SCALAR_PIECES[b], PASS)
+                    prep_quantize(b, 1)
+                if 1 <= at <= SCALAR_PIECES[b]:
+                    later[b][0]("scalar", prep[b, 0], 0, PIECE * (at - 1), PIECE * at)
+                if at == SCALAR_PIECES[b] + 1:
+                    prep_quantize(b, 0)
+            done = s - LAG - PACK
+            if done >= 0 and done % PACK == 0:
+                a_weave(done // PACK)
+            if done >= 0 and done % PACK == 1:
+                a_quantize(done // PACK)
+            for j in range(2):
+                if s == T_FIRST + 2 * j:
+                    t_banks[j] = t_matmuls(j)
+                if s == T_FIRST + 2 * j + 1:
+                    t_woven[j] = t_copy(t_banks[j], T0_ENG)
+                if s == T_FIRST + 2 * j + 2:
+                    t_quantize(j, t_woven[j])
+            if s == len(slots) - 1:
+                means[0, 0] = mean_matmuls(0, 0)
+
+        def halves(i):
+            return [(j, lh) for j, lh in ((i, 0), (i - 1, 1)) if 0 <= j < TILES]
+
+        scaled, ys, y_bf, y_woven = {}, {}, {}, {}
+
+        def apply_guide(k):
+            j, lh = k
+            scaled[k] = rotating("scaled", [P, PASS], F32, 3)
+            nc.vector.scalar_tensor_tensor(
+                out=scaled[k][:], in0=means[k][:], scalar=cols[:, TILES + j : TILES + j + 1],
+                in1=gd[j // 2][:, j % 2, PASS * lh : PASS * (lh + 1)], op0=ALU.mult, op1=ALU.mult,
+            )
+
+        def add_base(k):
+            j, lh = k
+            ys[k] = rotating("y", [P, PASS], F32, 6)
+            nc.vector.tensor_tensor(
+                out=ys[k][:], in0=scaled[k][:], in1=bs[j // 2][:, j % 2, PASS * lh : PASS * (lh + 1)], op=ALU.add
+            )
+            nc.sync.dma_start(out=out_0[P * j : P * (j + 1), PASS * lh : PASS * (lh + 1)], in_=ys[k][:])
+
+        def round_y(k):
+            y_bf[k] = rotating("y_bf", [P, PASS], BF16, 4)
+            nc.scalar.copy(
+                out=y_bf[k][:].rearrange("n (u p e) -> n u p e", u=2, e=2),
+                in_=ys[k][:].rearrange("n (p u e) -> n u p e", u=2, e=2),
+            )
+
+        def turn_y(ks):
+            acc = bank()
+            for i, k in enumerate(ks):
+                for u in range(2):
+                    nc.tensor.transpose(
+                        acc[:, P * (2 * i + u) : P * (2 * i + u + 1)],
+                        y_bf[k][:].bitcast(F32)[:, P * u : P * (u + 1)], ident[:],
+                    )
+            return acc
+
+        def y_copy(ks, acc):
+            for i, k in enumerate(ks):
+                y_woven[k] = rotating("y_woven", [P, PASS], BF16, 4)
+                nc.scalar.copy(
+                    out=y_woven[k][:].bitcast(F32).rearrange("p (n u) -> p n u", u=2),
+                    in_=acc[:, 2 * P * i : 2 * P * (i + 1)].rearrange("p (u n) -> p n u", u=2),
+                )
+
+        def y_quantize(k):
+            j, lh = k
+            words = y_words[lh, j // WORD_TILES]
+            at = P * (j % WORD_TILES)
+            quantize(words[:, at : at + P], y_scales[:, lh, P * j : P * (j + 1)], y_woven[k][:])
+            if j % WORD_TILES == WORD_TILES - 1:
+                first = P * (j + 1 - WORD_TILES)
+                nc.sync.dma_start(
+                    out=out_1[lh].rearrange("p m t -> p (m t)")[:, PACK * first : PACK * P * (j + 1)].bitcast(I32),
+                    in_=words[:].bitcast(I32),
+                )
+
+        for i in range(TILES + 3):
+            ahead = i + 2
+            if ahead < TILES:
+                t_banks[ahead] = t_matmuls(ahead)
+            for k in halves(i - 1):
+                round_y(k)
+            if halves(i - 1):
+                turned = turn_y(halves(i - 1))
+            for k in halves(i):
+                apply_guide(k)
+            if i == 0:
+                a_weave(len(units) - 1, LAST_SCALAR)
+            if ahead < TILES:
+                t_woven[ahead] = t_copy(t_banks[ahead])
+            for k in halves(i)[:-1]:
+                add_base(k)
+            for k in halves(i - 2):
+                y_quantize(k)
+            for k in halves(i)[-1:]:
+                add_base(k)
+            if i == 0:
+                a_quantize(len(units) - 1)
+            for k in halves(i + 1):
+                means[k] = mean_matmuls(k[0], k[1])
+            if halves(i - 1):
+                y_copy(halves(i - 1), turned)
+            if ahead < TILES:
+                t_quantize(ahead, t_woven[ahead])
+
+        for q in range(4):
+            (nc.scalar if q % 2 else nc.sync).dma_start(
+                out=out_2[:, 4 * q : 4 * q + 4, :].rearrange("g r m -> r g m").bitcast(I32),
+                in_=y_scales[32 * q : 32 * q + 4].bitcast(I32),
+            )

@@ -22,15 +22,24 @@ PASS = P * PACK
 GROUPS = N // PASS
 TILES = N // P
 PIECE = 128
-SCALAR_PIECES = (3, 3, 2)
+SCALAR_PIECES = (0, 3, 3)
 HEAD_SCALAR = 192
 LAST_SCALAR = 128
 T0_ENG = ("scalar", "scalar")
-T_FIRST = 11
+T_FIRST = 6
+T_STEP = 3
+SQ_FIRST = 3
+A_FIRST = 8
+A_STEP = 3
+A_SCALAR = 0
+SORT_AT = 2
 LAG = 2
-BL_FIRST = 1
+AHEAD = 4
+BL_FIRST = 3
 BL_STEP = 3
 WORD_TILES = 2
+RING_A, RING_B, RING_T = (0, 1), (2, 3, 4), (5, 6, 7)
+RING_TURN, RING_MEAN = (0,), (1, 2, 3, 4)
 
 
 def tile_mean_free_guided_pass_k4_kernel(
@@ -42,7 +51,7 @@ def tile_mean_free_guided_pass_k4_kernel(
         keep = ctx.enter_context(tc.tile_pool(name="keep", bufs=1))
         work = ctx.enter_context(tc.tile_pool(name="work", bufs=2))
         psum = ctx.enter_context(tc.psum_pool(name="psum", bufs=8))
-        ctx.enter_context(tc.manual_schedule())
+        ctx.enter_context(tc.manual_schedule(engines={mybir.EngineType.SP}))
 
         def kept(name, shape, dtype):
             return keep.tile(shape, dtype, name=name, align_bytes=64)
@@ -50,8 +59,9 @@ def tile_mean_free_guided_pass_k4_kernel(
         def rotating(tag, shape, dtype, bufs):
             return work.tile(shape, dtype, name=tag, tag=tag, bufs=bufs, align_bytes=64)
 
-        def bank():
-            return psum.tile([P, PASS], F32, name="bank", tag="bank")
+        def bank(ring, count):
+            name = "bank"
+            return psum.tile([P, PASS], F32, name=name, tag=name)
 
         v_words = [kept("v_words%d" % h, [P, GROUPS, N], U8) for h in range(2)]
         v_scales = kept("v_scales", [P, GROUPS, N], U8)
@@ -60,9 +70,9 @@ def tile_mean_free_guided_pass_k4_kernel(
         c_scales = kept("c_scales", [P, GROUPS, L], U8)
         c_words = [kept("c_words%d" % lh, [P, GROUPS, PASS], U32) for lh in range(2)]
         sq_raw = {(g, lh): kept("sq_raw%d%d" % (g, lh), [P, PACK, PASS], BF16) for g in range(2) for lh in range(2)}
-        bl_raw = {(g, h): kept("bl_raw%d%d" % (g, h), [P, PACK, PASS], BF16) for g in range(2) for h in range(2)}
-        gd = [kept("guide%d" % i, [P, 2, L], BF16) for i in range(TILES // 2)]
-        bs = [kept("base%d" % i, [P, 2, L], BF16) for i in range(TILES // 2)]
+        bl_raw = [kept("bl_raw%d" % g, [P, PACK, N], BF16) for g in range(2)]
+        gd = kept("guide", [P, TILES * L], BF16)
+        bs = kept("base", [P, TILES * L], BF16)
         pairs = [(a, b) for a in range(2) for b in range(2)]
         sq_q = {k: (kept("sq_c%d%d" % k, [P, PASS], U32), kept("sq_s%d%d" % k, [P, PASS], U8)) for k in pairs}
         bl_q = {k: (kept("bl_c%d%d" % k, [P, PASS], U32), kept("bl_s%d%d" % k, [P, PASS], U8)) for k in pairs}
@@ -80,6 +90,9 @@ def tile_mean_free_guided_pass_k4_kernel(
 
         warm = kept("warm", [P, 2], F32)
 
+        make_identity(nc, ident[:])
+        nc.gpsimd.tensor_copy(out=ident_bf[:], in_=ident[:, 0:TILES])
+        nc.gpsimd.memset(rows[:], 0.0)
         nc.vector.memset(v_scales[:].rearrange("p g n -> p (g n)").bitcast(I32), 0)
         nc.vector.memset(c_scales[:].rearrange("p g n -> p (g n)").bitcast(I32), 0)
 
@@ -108,34 +121,34 @@ def tile_mean_free_guided_pass_k4_kernel(
                 in_=win_words.rearrange("g p b -> p g b")[:, :, N * h : N * (h + 1)].bitcast(I32),
             )
 
+        def load_blend(g):
+            nc.sync.dma_start(
+                out=bl_raw[g][:], in_=blend[PASS * g : PASS * (g + 1), :].rearrange("(p j) c -> p j c", j=PACK)
+            )
+
         load_window(0)
         load_rows(sq_raw, square, 0, 0)
         load_scales(v_scales, win_scales)
         load_rows(sq_raw, square, 1, 0)
-        load_rows(sq_raw, square, 0, 1)
+        load_blend(1)
         load_scales(c_scales, cross_scales)
-        load_rows(sq_raw, square, 1, 1)
         load_cross(0)
+        nc.sync.dma_start(
+            out=rows[0:PACK, 0 : 2 * P].rearrange("t (m r) -> t m r", r=4),
+            in_=conf.rearrange("(m t r) -> t m r", t=PACK, r=4),
+        )
+        nc.sync.dma_start(out=rows[0:TILES, 2 * P : 3 * P], in_=norm.rearrange("(j p) -> j p", p=P))
         load_window(1)
-        load_rows(bl_raw, blend, 1, 0)
-        load_rows(bl_raw, blend, 0, 0)
-        load_rows(bl_raw, blend, 1, 1)
-        load_rows(bl_raw, blend, 0, 1)
+        load_blend(0)
+        load_rows(sq_raw, square, 0, 1)
+        load_rows(sq_raw, square, 1, 1)
         load_cross(1)
         for i in range(TILES // 2):
             for dst, src in ((gd, guide), (bs, base)):
                 nc.sync.dma_start(
-                    out=dst[i][:], in_=src[2 * P * i : 2 * P * (i + 1), :].rearrange("(j p) l -> p j l", p=P)
+                    out=dst[:, 2 * L * i : 2 * L * (i + 1)].rearrange("p (j l) -> p j l", j=2),
+                    in_=src[2 * P * i : 2 * P * (i + 1), :].rearrange("(j p) l -> p j l", p=P),
                 )
-
-        nc.gpsimd.memset(rows[:], 0.0)
-        nc.gpsimd.dma_start(
-            out=rows[0:PACK, 0 : 2 * P].rearrange("t (m r) -> t m r", r=4),
-            in_=conf.rearrange("(m t r) -> t m r", t=PACK, r=4),
-        )
-        nc.gpsimd.dma_start(out=rows[0:TILES, 2 * P : 3 * P], in_=norm.rearrange("(j p) -> j p", p=P))
-        make_identity(nc, ident[:])
-        nc.gpsimd.tensor_copy(out=ident_bf[:], in_=ident[:, 0:TILES])
 
         def copy_on(engine, out, in_):
             if engine == "scalar":
@@ -158,7 +171,7 @@ def tile_mean_free_guided_pass_k4_kernel(
             copy_on(
                 engine,
                 woven[:].rearrange("p (t m r j) -> p m t j r", t=PACK, r=4, j=PACK)[:, :, slots_here],
-                raw[:].rearrange("p j (m t r) -> p m t j r", t=PACK, r=4)[:, :, slots_here],
+                raw.rearrange("p j (m t r) -> p m t j r", t=PACK, r=4)[:, :, slots_here],
             )
 
         def new_woven():
@@ -183,22 +196,24 @@ def tile_mean_free_guided_pass_k4_kernel(
         quantize(sq_q[0, 0][0][:], sq_q[0, 0][1][:], head[0][:])
         weave_rows("scalar", head[1], sq_raw[1, 0], 0, HEAD_SCALAR)
         weave_rows("vector", head[1], sq_raw[1, 0], HEAD_SCALAR, PASS)
-        col_bank = bank()
-        for h in range(2):
-            nc.tensor.matmul(
-                col_bank[:, PACK * h : PACK * (h + 1)], lhsT=rows[:, P * h : P * (h + 1)], rhs=ident_bf[:, 0:PACK],
-                start=True, stop=True,
-            )
-        nc.tensor.matmul(
-            col_bank[:, TILES : 2 * TILES], lhsT=rows[:, 2 * P : 3 * P], rhs=ident_bf[:], start=True, stop=True
-        )
         quantize(sq_q[1, 0][0][:], sq_q[1, 0][1][:], head[1][:])
-        nc.scalar.copy(out=cols[:], in_=col_bank[:, 0 : 2 * TILES])
 
-        def moment(s, operand):
+        def line_columns():
+            col_bank = bank(RING_T, 2)
+            for h in range(2):
+                nc.tensor.matmul(
+                    col_bank[:, PACK * h : PACK * (h + 1)], lhsT=rows[:, P * h : P * (h + 1)], rhs=ident_bf[:, 0:PACK],
+                    start=True, stop=True,
+                )
+            nc.tensor.matmul(
+                col_bank[:, TILES : 2 * TILES], lhsT=rows[:, 2 * P : 3 * P], rhs=ident_bf[:], start=True, stop=True
+            )
+            nc.scalar.copy(out=cols[:], in_=col_bank[:, 0 : 2 * TILES])
+
+        def moment(s, operand, ring):
             (h, lh), t = units[slots[s][0]], slots[s][1]
             slot = PACK * h + t
-            acc = bank()
+            acc = bank(ring, s)
             for g in range(GROUPS):
                 codes, scales = operand(g, lh)
                 nc.tensor.matmul_mx(
@@ -217,7 +232,7 @@ def tile_mean_free_guided_pass_k4_kernel(
             return c_words[lh][:, g, :], c_scales[:, g, PASS * lh : PASS * (lh + 1)]
 
         def t_matmuls(j):
-            banks = [bank(), bank()]
+            banks = [bank(RING_T, 2 * j + h) for h in range(2)]
             for h in range(2):
                 for t in range(PACK):
                     for g in range(GROUPS):
@@ -232,7 +247,7 @@ def tile_mean_free_guided_pass_k4_kernel(
             return banks
 
         def t_copy(banks, engines=("scalar", "scalar")):
-            woven = rotating("t_woven", [P, 2 * PASS], BF16, 2)
+            woven = rotating("t_woven", [P, 2 * PASS], BF16, 3)
             for h in range(2):
                 copy_on(
                     engines[h],
@@ -244,8 +259,9 @@ def tile_mean_free_guided_pass_k4_kernel(
         def t_quantize(j, woven):
             quantize(t_q[j][0][:], t_q[j][1][:], woven[:])
 
-        def mean_matmuls(j, lh):
-            acc = bank()
+        def mean_matmuls(q):
+            j, lh = divmod(q, 2)
+            acc = bank(RING_MEAN, q)
             for h in range(2):
                 nc.tensor.matmul_mx(
                     out=acc[:],
@@ -260,8 +276,8 @@ def tile_mean_free_guided_pass_k4_kernel(
         slots = [(u, t) for u in range(len(units)) for t in range(PACK)]
         later = [
             (lambda e, w, g, c0, c1: weave_rows(e, w, sq_raw[g, 1], c0, c1), lambda g: sq_q[g, 1]),
-            (lambda e, w, g, c0, c1: weave_blend(e, w, bl_raw[g, 0], c0, c1), lambda g: bl_q[g, 0]),
-            (lambda e, w, g, c0, c1: weave_blend(e, w, bl_raw[g, 1], c0, c1), lambda g: bl_q[g, 1]),
+            (lambda e, w, g, c0, c1: weave_blend(e, w, bl_raw[g][:, :, 0:PASS], c0, c1), lambda g: bl_q[g, 0]),
+            (lambda e, w, g, c0, c1: weave_blend(e, w, bl_raw[g][:, :, PASS:N], c0, c1), lambda g: bl_q[g, 1]),
         ]
         root, recip, nums, a_rows, a_woven, prep, t_banks, t_woven = {}, {}, {}, {}, {}, {}, {}, {}
 
@@ -272,7 +288,7 @@ def tile_mean_free_guided_pass_k4_kernel(
         def ratio(s):
             u, t = slots[s]
             if t == 0:
-                a_rows[u] = rotating("a_rows", [P, PACK, PASS], BF16, 2)
+                a_rows[u] = rotating("a_rows", [P, PACK, PASS], BF16, 3)
             slot = PACK * units[u][0] + t
             nc.vector.scalar_tensor_tensor(
                 out=a_rows[u][:, t, :], in0=nums[s][:], scalar=cols[:, slot : slot + 1], in1=recip[s][:],
@@ -292,138 +308,143 @@ def tile_mean_free_guided_pass_k4_kernel(
             codes, scales = later[u][1](g)
             quantize(codes[:], scales[:], prep[u, g][:])
 
-        prep[0, 0], prep[0, 1] = new_woven(), new_woven()
-        later[0][0]("scalar", prep[0, 0], 0, 0, PIECE * SCALAR_PIECES[0])
         means = {}
+        blend_order = [(g, h) for g in reversed(range(GROUPS)) for h in range(2)]
         for s in range(len(slots) + LAG):
             if s < len(slots):
-                den = moment(s, square_operand)
+                den = moment(s, square_operand, RING_A)
+                nums[s] = moment(s, cross_operand, RING_B)
                 root[s] = rotating("root", [P, PASS], F32, 2)
                 nc.scalar.activation(out=root[s][:], in_=den[:], func=ACT.Abs_reciprocal_sqrt)
+            if s == 0:
+                line_columns()
             if 0 < s <= len(slots):
-                nums[s - 1] = moment(s - 1, cross_operand)
                 square_root_step(s - 1)
             if s >= LAG:
                 ratio(s - LAG)
-            if s == 0:
-                later[0][0]("vector", prep[0, 0], 0, PIECE * SCALAR_PIECES[0], PASS)
-                later[0][0]("vector", prep[0, 1], 1, 0, PASS)
-                prep_quantize(0, 0)
+            if s < len(blend_order):
+                g, h = blend_order[s]
+                prep[1 + h, g] = new_woven()
+                later[1 + h][0]("vector", prep[1 + h, g], g, 0, PASS)
+            if 0 < s <= len(blend_order):
+                g, h = blend_order[s - 1]
+                prep_quantize(1 + h, g)
+            if s == SORT_AT:
                 sort_window(1)
+            at = s - SQ_FIRST
+            if at == 0:
+                prep[0, 0], prep[0, 1] = new_woven(), new_woven()
+            if 0 <= at < PACK:
+                later[0][0]("scalar", prep[0, 0], 0, PIECE * at, PIECE * (at + 1))
+            if at == 2:
+                later[0][0]("vector", prep[0, 1], 1, 0, PASS)
+            if at == 3:
                 prep_quantize(0, 1)
-            for b in (1, 2):
-                at = s - (BL_FIRST + BL_STEP * (b - 1))
-                if at == 0:
-                    prep[b, 0], prep[b, 1] = new_woven(), new_woven()
-                    later[b][0]("vector", prep[b, 1], 1, 0, PASS)
-                if at == 1:
-                    later[b][0]("vector", prep[b, 0], 0, PIECE * SCALAR_PIECES[b], PASS)
-                    prep_quantize(b, 1)
-                if 1 <= at <= SCALAR_PIECES[b]:
-                    later[b][0]("scalar", prep[b, 0], 0, PIECE * (at - 1), PIECE * at)
-                if at == SCALAR_PIECES[b] + 1:
-                    prep_quantize(b, 0)
-            done = s - LAG - PACK
-            if done >= 0 and done % PACK == 0:
-                a_weave(done // PACK)
-            if done >= 0 and done % PACK == 1:
-                a_quantize(done // PACK)
-            for j in range(2):
-                if s == T_FIRST + 2 * j:
-                    t_banks[j] = t_matmuls(j)
-                if s == T_FIRST + 2 * j + 1:
-                    t_woven[j] = t_copy(t_banks[j], T0_ENG)
-                if s == T_FIRST + 2 * j + 2:
+            if at == PACK:
+                prep_quantize(0, 0)
+            for u in range(len(units) - 1):
+                if s == A_FIRST + A_STEP * u:
+                    a_weave(u, A_SCALAR)
+                if s == A_FIRST + A_STEP * u + 1:
+                    a_quantize(u)
+            for j in range(AHEAD):
+                if s == T_FIRST + T_STEP * j + 2 and j < AHEAD - 2:
                     t_quantize(j, t_woven[j])
-            if s == len(slots) - 1:
-                means[0, 0] = mean_matmuls(0, 0)
+                if s == T_FIRST + T_STEP * j + 1 and j < AHEAD - 1:
+                    t_woven[j] = t_copy(t_banks[j])
+                if s == T_FIRST + T_STEP * j:
+                    t_banks[j] = t_matmuls(j)
+            if s == len(slots):
+                means[0] = mean_matmuls(0)
 
         def halves(i):
-            return [(j, lh) for j, lh in ((i, 0), (i - 1, 1)) if 0 <= j < TILES]
+            return [q for q in (2 * i - 1, 2 * i) if 0 <= q < 2 * TILES]
 
-        scaled, ys, y_bf, y_woven = {}, {}, {}, {}
+        scaled, ys, y_bf, y_woven, turned = {}, {}, {}, {}, {}
 
-        def apply_guide(k):
-            j, lh = k
-            scaled[k] = rotating("scaled", [P, PASS], F32, 3)
-            nc.vector.scalar_tensor_tensor(
-                out=scaled[k][:], in0=means[k][:], scalar=cols[:, TILES + j : TILES + j + 1],
-                in1=gd[j // 2][:, j % 2, PASS * lh : PASS * (lh + 1)], op0=ALU.mult, op1=ALU.mult,
-            )
+        def apply_guide(i):
+            scaled[i] = rotating("scaled", [P, L], F32, 2)
+            for x, q in reversed(list(enumerate(halves(i)))):
+                nc.vector.scalar_tensor_tensor(
+                    out=scaled[i][:, PASS * x : PASS * (x + 1)], in0=means[q][:],
+                    scalar=cols[:, TILES + q // 2 : TILES + q // 2 + 1],
+                    in1=gd[:, PASS * q : PASS * (q + 1)], op0=ALU.mult, op1=ALU.mult,
+                )
 
-        def add_base(k):
-            j, lh = k
-            ys[k] = rotating("y", [P, PASS], F32, 6)
+        def add_base(i):
+            first, width = PASS * halves(i)[0], PASS * len(halves(i))
+            ys[i] = rotating("y", [P, L], F32, 4)
             nc.vector.tensor_tensor(
-                out=ys[k][:], in0=scaled[k][:], in1=bs[j // 2][:, j % 2, PASS * lh : PASS * (lh + 1)], op=ALU.add
+                out=ys[i][:, 0:width], in0=scaled[i][:, 0:width], in1=bs[:, first : first + width], op=ALU.add
             )
-            nc.sync.dma_start(out=out_0[P * j : P * (j + 1), PASS * lh : PASS * (lh + 1)], in_=ys[k][:])
-
-        def round_y(k):
-            y_bf[k] = rotating("y_bf", [P, PASS], BF16, 4)
-            nc.scalar.copy(
-                out=y_bf[k][:].rearrange("n (u p e) -> n u p e", u=2, e=2),
-                in_=ys[k][:].rearrange("n (p u e) -> n u p e", u=2, e=2),
-            )
-
-        def turn_y(ks):
-            acc = bank()
-            for i, k in enumerate(ks):
-                for u in range(2):
-                    nc.tensor.transpose(
-                        acc[:, P * (2 * i + u) : P * (2 * i + u + 1)],
-                        y_bf[k][:].bitcast(F32)[:, P * u : P * (u + 1)], ident[:],
-                    )
-            return acc
-
-        def y_copy(ks, acc):
-            for i, k in enumerate(ks):
-                y_woven[k] = rotating("y_woven", [P, PASS], BF16, 4)
-                nc.scalar.copy(
-                    out=y_woven[k][:].bitcast(F32).rearrange("p (n u) -> p n u", u=2),
-                    in_=acc[:, 2 * P * i : 2 * P * (i + 1)].rearrange("p (u n) -> p n u", u=2),
-                )
-
-        def y_quantize(k):
-            j, lh = k
-            words = y_words[lh, j // WORD_TILES]
-            at = P * (j % WORD_TILES)
-            quantize(words[:, at : at + P], y_scales[:, lh, P * j : P * (j + 1)], y_woven[k][:])
-            if j % WORD_TILES == WORD_TILES - 1:
-                first = P * (j + 1 - WORD_TILES)
+            for x, q in enumerate(halves(i)):
+                j, lh = divmod(q, 2)
                 nc.sync.dma_start(
-                    out=out_1[lh].rearrange("p m t -> p (m t)")[:, PACK * first : PACK * P * (j + 1)].bitcast(I32),
-                    in_=words[:].bitcast(I32),
+                    out=out_0[P * j : P * (j + 1), PASS * lh : PASS * (lh + 1)], in_=ys[i][:, PASS * x : PASS * (x + 1)]
                 )
 
-        for i in range(TILES + 3):
-            ahead = i + 2
-            if ahead < TILES:
-                t_banks[ahead] = t_matmuls(ahead)
-            for k in halves(i - 1):
-                round_y(k)
-            if halves(i - 1):
-                turned = turn_y(halves(i - 1))
-            for k in halves(i):
-                apply_guide(k)
+        def round_y(i):
+            width = PASS * len(halves(i))
+            y_bf[i] = rotating("y_bf", [P, L], BF16, 2)
+            nc.scalar.copy(
+                out=y_bf[i][:, 0:width].rearrange("n (x u p e) -> n x u p e", u=2, p=P, e=2),
+                in_=ys[i][:, 0:width].rearrange("n (x p u e) -> n x u p e", u=2, p=P, e=2),
+            )
+
+        def turn_y(i):
+            turned[i] = bank(RING_TURN, i)
+            for b in range(2 * len(halves(i))):
+                nc.tensor.transpose(
+                    turned[i][:, P * b : P * (b + 1)], y_bf[i][:].bitcast(F32)[:, P * b : P * (b + 1)], ident[:]
+                )
+
+        def y_copy(i):
+            words = 2 * P * len(halves(i))
+            y_woven[i] = rotating("y_woven", [P, L], BF16, 2)
+            nc.scalar.copy(
+                out=y_woven[i][:].bitcast(F32)[:, 0:words].rearrange("p (x n u) -> p x n u", n=P, u=2),
+                in_=turned[i][:, 0:words].rearrange("p (x u n) -> p x n u", n=P, u=2),
+            )
+
+        def y_quantize(i):
+            for x, q in enumerate(halves(i)):
+                j, lh = divmod(q, 2)
+                words = y_words[lh, j // WORD_TILES]
+                at = P * (j % WORD_TILES)
+                quantize(words[:, at : at + P], y_scales[:, lh, P * j : P * (j + 1)], y_woven[i][:, PASS * x : PASS * (x + 1)])
+                if j % WORD_TILES == WORD_TILES - 1:
+                    first = P * (j + 1 - WORD_TILES)
+                    nc.sync.dma_start(
+                        out=out_1[lh].rearrange("p m t -> p (m t)")[:, PACK * first : PACK * P * (j + 1)].bitcast(I32),
+                        in_=words[:].bitcast(I32),
+                    )
+
+        steps = TILES + 1
+        for i in range(steps + 3):
+            if i < steps:
+                apply_guide(i)
             if i == 0:
                 a_weave(len(units) - 1, LAST_SCALAR)
-            if ahead < TILES:
-                t_woven[ahead] = t_copy(t_banks[ahead])
-            for k in halves(i)[:-1]:
-                add_base(k)
-            for k in halves(i - 2):
-                y_quantize(k)
-            for k in halves(i)[-1:]:
-                add_base(k)
+            if i + AHEAD - 1 < TILES:
+                t_woven[i + AHEAD - 1] = t_copy(t_banks[i + AHEAD - 1])
+            if i + AHEAD - 2 < TILES:
+                t_quantize(i + AHEAD - 2, t_woven[i + AHEAD - 2])
             if i == 0:
                 a_quantize(len(units) - 1)
-            for k in halves(i + 1):
-                means[k] = mean_matmuls(k[0], k[1])
-            if halves(i - 1):
-                y_copy(halves(i - 1), turned)
-            if ahead < TILES:
-                t_quantize(ahead, t_woven[ahead])
+            if 3 <= i < steps + 3:
+                y_quantize(i - 3)
+            if 2 <= i < steps + 2:
+                turn_y(i - 2)
+            if 2 <= i < steps + 2:
+                y_copy(i - 2)
+            if i < steps:
+                add_base(i)
+            if i + AHEAD < TILES:
+                t_banks[i + AHEAD] = t_matmuls(i + AHEAD)
+            for q in reversed(halves(i + 1)):
+                means[q] = mean_matmuls(q)
+            if 1 <= i <= steps:
+                round_y(i - 1)
 
         for q in range(4):
             (nc.scalar if q % 2 else nc.sync).dma_start(

@@ -15,6 +15,7 @@ FP8X4 = mybir.dt.float8_e4m3fn_x4
 FP4X4 = mybir.dt.float4_e2m1fn_x4
 ACT = mybir.ActivationFunctionType
 ALU = mybir.AluOpType
+ENG = mybir.EngineType
 
 P = 128
 PACK = 4
@@ -26,20 +27,25 @@ SCALAR_PIECES = (0, 3, 3)
 HEAD_SCALAR = 192
 LAST_SCALAR = 128
 T0_ENG = ("scalar", "scalar")
-T_FIRST = 6
-T_STEP = 3
-SQ_FIRST = 3
+T_FIRST = 10
+GP_WEAVE = (192, 192, 192, 128)
+SCALAR_SHARE = 3
+T_EARLY = 3
+SQ_FIRST = 4
 A_FIRST = 8
 A_STEP = 3
 A_SCALAR = 0
-SORT_AT = 2
+SORT_AT = 1
 LAG = 2
+GP_ADD = 384
+GP_FROM = 1
+GP_TO = 1
+EARLY = 4
 AHEAD = 4
 BL_FIRST = 3
 BL_STEP = 3
 WORD_TILES = 2
-RING_A, RING_B, RING_T = (0, 1), (2, 3, 4), (5, 6, 7)
-RING_TURN, RING_MEAN = (0,), (1, 2, 3, 4)
+RING_A, RING_B, RING_T = (0, 1), (2, 3, 4, 5), (6, 7)
 
 
 def tile_mean_free_guided_pass_k4_kernel(
@@ -50,8 +56,8 @@ def tile_mean_free_guided_pass_k4_kernel(
     with ExitStack() as ctx:
         keep = ctx.enter_context(tc.tile_pool(name="keep", bufs=1))
         work = ctx.enter_context(tc.tile_pool(name="work", bufs=2))
-        psum = ctx.enter_context(tc.psum_pool(name="psum", bufs=8))
-        ctx.enter_context(tc.manual_schedule(engines={mybir.EngineType.SP}))
+        psum = ctx.enter_context(tc.psum_pool(name="psum", bufs=1))
+        ctx.enter_context(tc.manual_schedule(engines={ENG.SP, ENG.DVE, ENG.Pool}))
 
         def kept(name, shape, dtype):
             return keep.tile(shape, dtype, name=name, align_bytes=64)
@@ -60,7 +66,7 @@ def tile_mean_free_guided_pass_k4_kernel(
             return work.tile(shape, dtype, name=tag, tag=tag, bufs=bufs, align_bytes=64)
 
         def bank(ring, count):
-            name = "bank"
+            name = "bank%d" % ring[count % len(ring)]
             return psum.tile([P, PASS], F32, name=name, tag=name)
 
         v_words = [kept("v_words%d" % h, [P, GROUPS, N], U8) for h in range(2)]
@@ -82,7 +88,7 @@ def tile_mean_free_guided_pass_k4_kernel(
             (lh, i): kept("y_words%d%d" % (lh, i), [P, WORD_TILES * P], U32)
             for lh in range(2) for i in range(TILES // WORD_TILES)
         }
-        y_scales = kept("y_scales", [P, 2, N], U8)
+        y_scales = [kept("y_scales0", [P, 2, EARLY * P], U8), kept("y_scales1", [P, 2, N - EARLY * P], U8)]
         rows = kept("rows", [P, 3 * P], BF16)
         ident = kept("ident", [P, P], F32)
         ident_bf = kept("ident_bf", [P, TILES], BF16)
@@ -126,22 +132,22 @@ def tile_mean_free_guided_pass_k4_kernel(
                 out=bl_raw[g][:], in_=blend[PASS * g : PASS * (g + 1), :].rearrange("(p j) c -> p j c", j=PACK)
             )
 
-        load_window(0)
         load_rows(sq_raw, square, 0, 0)
-        load_scales(v_scales, win_scales)
         load_rows(sq_raw, square, 1, 0)
-        load_blend(1)
-        load_scales(c_scales, cross_scales)
-        load_cross(0)
+        load_window(0)
+        load_scales(v_scales, win_scales)
+        load_rows(sq_raw, square, 0, 1)
         nc.sync.dma_start(
             out=rows[0:PACK, 0 : 2 * P].rearrange("t (m r) -> t m r", r=4),
             in_=conf.rearrange("(m t r) -> t m r", t=PACK, r=4),
         )
         nc.sync.dma_start(out=rows[0:TILES, 2 * P : 3 * P], in_=norm.rearrange("(j p) -> j p", p=P))
+        load_scales(c_scales, cross_scales)
+        load_cross(0)
         load_window(1)
-        load_blend(0)
-        load_rows(sq_raw, square, 0, 1)
         load_rows(sq_raw, square, 1, 1)
+        load_blend(1)
+        load_blend(0)
         load_cross(1)
         for i in range(TILES // 2):
             for dst, src in ((gd, guide), (bs, base)):
@@ -153,6 +159,8 @@ def tile_mean_free_guided_pass_k4_kernel(
         def copy_on(engine, out, in_):
             if engine == "scalar":
                 nc.scalar.copy(out=out, in_=in_)
+            elif engine == "gpsimd":
+                nc.gpsimd.tensor_scalar(out=out, in0=in_, scalar1=1.0, scalar2=1.0, op0=ALU.mult, op1=ALU.mult)
             else:
                 nc.vector.tensor_copy(out=out, in_=in_)
 
@@ -186,7 +194,6 @@ def tile_mean_free_guided_pass_k4_kernel(
                 in_=v_words[h][:].bitcast(I32).rearrange("p g (m t w) -> p g t m w", t=PACK, w=2),
             )
 
-        sort_window(0)
         weave_rows("scalar", head[0], sq_raw[0, 0], 0, HEAD_SCALAR)
         weave_rows("vector", head[0], sq_raw[0, 0], HEAD_SCALAR, PASS)
         nc.vector.tensor_copy(
@@ -196,10 +203,11 @@ def tile_mean_free_guided_pass_k4_kernel(
         quantize(sq_q[0, 0][0][:], sq_q[0, 0][1][:], head[0][:])
         weave_rows("scalar", head[1], sq_raw[1, 0], 0, HEAD_SCALAR)
         weave_rows("vector", head[1], sq_raw[1, 0], HEAD_SCALAR, PASS)
+        sort_window(0)
         quantize(sq_q[1, 0][0][:], sq_q[1, 0][1][:], head[1][:])
 
         def line_columns():
-            col_bank = bank(RING_T, 2)
+            col_bank = bank(RING_T, 1)
             for h in range(2):
                 nc.tensor.matmul(
                     col_bank[:, PACK * h : PACK * (h + 1)], lhsT=rows[:, P * h : P * (h + 1)], rhs=ident_bf[:, 0:PACK],
@@ -259,9 +267,9 @@ def tile_mean_free_guided_pass_k4_kernel(
         def t_quantize(j, woven):
             quantize(t_q[j][0][:], t_q[j][1][:], woven[:])
 
-        def mean_matmuls(q):
+        def mean_matmuls(q, count):
             j, lh = divmod(q, 2)
-            acc = bank(RING_MEAN, q)
+            acc = bank(RING_B, count)
             for h in range(2):
                 nc.tensor.matmul_mx(
                     out=acc[:],
@@ -282,24 +290,25 @@ def tile_mean_free_guided_pass_k4_kernel(
         root, recip, nums, a_rows, a_woven, prep, t_banks, t_woven = {}, {}, {}, {}, {}, {}, {}, {}
 
         def square_root_step(s):
-            recip[s] = rotating("recip", [P, PASS], F32, 4)
+            recip[s] = rotating("recip", [P, PASS], F32, 5)
             nc.scalar.activation(out=recip[s][:], in_=root[s][:], func=ACT.Square)
 
         def ratio(s):
             u, t = slots[s]
             if t == 0:
-                a_rows[u] = rotating("a_rows", [P, PACK, PASS], BF16, 3)
+                a_rows[u] = rotating("a_rows", [P, PACK, PASS], BF16, 2)
             slot = PACK * units[u][0] + t
             nc.vector.scalar_tensor_tensor(
                 out=a_rows[u][:, t, :], in0=nums[s][:], scalar=cols[:, slot : slot + 1], in1=recip[s][:],
                 op0=ALU.mult, op1=ALU.mult,
             )
 
-        def a_weave(u, scalar_columns=0):
+        def a_weave_first(u):
             a_woven[u] = rotating("a_woven", [P, PACK * PASS], BF16, 2)
-            if scalar_columns:
-                weave_rows("scalar", a_woven[u], a_rows[u], 0, scalar_columns)
-            weave_rows("vector", a_woven[u], a_rows[u], scalar_columns, PASS)
+            weave_rows("gpsimd", a_woven[u], a_rows[u], 0, GP_WEAVE[u])
+
+        def a_weave_rest(u):
+            weave_rows("vector", a_woven[u], a_rows[u], GP_WEAVE[u], PASS)
 
         def a_quantize(u):
             quantize(a_q[units[u]][0][:], a_q[units[u]][1][:], a_woven[u][:])
@@ -308,146 +317,209 @@ def tile_mean_free_guided_pass_k4_kernel(
             codes, scales = later[u][1](g)
             quantize(codes[:], scales[:], prep[u, g][:])
 
-        means = {}
-        blend_order = [(g, h) for g in reversed(range(GROUPS)) for h in range(2)]
-        for s in range(len(slots) + LAG):
-            if s < len(slots):
-                den = moment(s, square_operand, RING_A)
+        def prep_weave(b, g):
+            prep[b, g] = new_woven()
+            later[b][0]("vector", prep[b, g], g, 0, PASS)
+
+        def t_step(s):
+            j, odd = divmod(s - T_FIRST, 2)
+            if 0 <= j < T_EARLY and odd:
+                t_woven[j] = t_copy(t_banks[j])
+            if 0 <= j < T_EARLY and not odd:
+                t_banks[j] = t_matmuls(j)
+
+        def between(b):
+            if b == 0:
+                prep_weave(0, 0)
+                sort_window(1)
+                prep_quantize(0, 0)
+            if b == 1:
+                prep_weave(0, 1)
+                prep_weave(1, 1)
+                prep_quantize(0, 1)
+                prep_weave(2, 1)
+                prep_quantize(1, 1)
+                prep_quantize(2, 1)
+            if b == 2:
+                prep_weave(1, 0)
+                if SCALAR_SHARE < PACK:
+                    later[2][0]("vector", prep[2, 0], 0, PIECE * SCALAR_SHARE, PASS)
+                a_weave_rest(0)
+                prep_quantize(1, 0)
+                prep_quantize(2, 0)
+                a_quantize(0)
+            if b == 3:
+                a_weave_rest(1)
+                t_quantize(0, t_woven[0])
+                a_quantize(1)
+
+        def ratios(b):
+            run = [s for s in range(PACK * b - 1, PACK * b + PACK - 1) if 0 <= s < len(slots)]
+            for s in run:
+                ratio(s)
+                if s % PACK == PACK - 1:
+                    a_weave_first(s // PACK)
+
+        between(0)
+        for s in range(len(slots)):
+            b, t = divmod(s, PACK)
+            den = moment(s, square_operand, RING_A)
+            if t < PACK - 1:
                 nums[s] = moment(s, cross_operand, RING_B)
-                root[s] = rotating("root", [P, PASS], F32, 2)
-                nc.scalar.activation(out=root[s][:], in_=den[:], func=ACT.Abs_reciprocal_sqrt)
+            root[s] = rotating("root", [P, PASS], F32, 2)
+            nc.scalar.activation(out=root[s][:], in_=den[:], func=ACT.Abs_reciprocal_sqrt)
             if s == 0:
                 line_columns()
-            if 0 < s <= len(slots):
+            if s > 0:
                 square_root_step(s - 1)
-            if s >= LAG:
-                ratio(s - LAG)
-            if s < len(blend_order):
-                g, h = blend_order[s]
-                prep[1 + h, g] = new_woven()
-                later[1 + h][0]("vector", prep[1 + h, g], g, 0, PASS)
-            if 0 < s <= len(blend_order):
-                g, h = blend_order[s - 1]
-                prep_quantize(1 + h, g)
-            if s == SORT_AT:
-                sort_window(1)
             at = s - SQ_FIRST
             if at == 0:
-                prep[0, 0], prep[0, 1] = new_woven(), new_woven()
-            if 0 <= at < PACK:
-                later[0][0]("scalar", prep[0, 0], 0, PIECE * at, PIECE * (at + 1))
-            if at == 2:
-                later[0][0]("vector", prep[0, 1], 1, 0, PASS)
-            if at == 3:
-                prep_quantize(0, 1)
-            if at == PACK:
-                prep_quantize(0, 0)
-            for u in range(len(units) - 1):
-                if s == A_FIRST + A_STEP * u:
-                    a_weave(u, A_SCALAR)
-                if s == A_FIRST + A_STEP * u + 1:
-                    a_quantize(u)
-            for j in range(AHEAD):
-                if s == T_FIRST + T_STEP * j + 2 and j < AHEAD - 2:
-                    t_quantize(j, t_woven[j])
-                if s == T_FIRST + T_STEP * j + 1 and j < AHEAD - 1:
-                    t_woven[j] = t_copy(t_banks[j])
-                if s == T_FIRST + T_STEP * j:
-                    t_banks[j] = t_matmuls(j)
-            if s == len(slots):
-                means[0] = mean_matmuls(0)
+                prep[2, 0] = new_woven()
+            if 0 <= at < SCALAR_SHARE:
+                later[2][0]("scalar", prep[2, 0], 0, PIECE * at, PIECE * (at + 1))
+            t_step(s)
+            if t == PACK - 1:
+                if b == 3:
+                    between(3)
+                ratios(b)
+                nums[s] = moment(s, cross_operand, RING_B)
+                if b < 2:
+                    between(b + 1)
+        square_root_step(len(slots) - 1)
 
-        def halves(i):
-            return [q for q in (2 * i - 1, 2 * i) if 0 <= q < 2 * TILES]
+        groups = [[0, 2], [1, 3, 4, 5], [6, 7, 8, 9], [10, 11, 12, 13], [14, 15]]
+        final = 2 * TILES - 1
+        means, ys, y_bf, y_woven, turned = {}, {}, {}, {}, {}
 
-        scaled, ys, y_bf, y_woven, turned = {}, {}, {}, {}, {}
+        def pieces(q, width):
+            return [(0, width // 2), (width // 2, width)] if q == final else [(0, width)]
+
+        def group_means(i):
+            for q in groups[i]:
+                means[q] = mean_matmuls(q, len(means))
 
         def apply_guide(i):
-            scaled[i] = rotating("scaled", [P, L], F32, 2)
-            for x, q in reversed(list(enumerate(halves(i)))):
-                nc.vector.scalar_tensor_tensor(
-                    out=scaled[i][:, PASS * x : PASS * (x + 1)], in0=means[q][:],
-                    scalar=cols[:, TILES + q // 2 : TILES + q // 2 + 1],
-                    in1=gd[:, PASS * q : PASS * (q + 1)], op0=ALU.mult, op1=ALU.mult,
-                )
+            ys[i] = rotating("y", [P, PACK * PASS], F32, 3)
+            for x, q in enumerate(groups[i]):
+                for c0, c1 in pieces(q, PASS):
+                    nc.vector.scalar_tensor_tensor(
+                        out=ys[i][:, PASS * x + c0 : PASS * x + c1], in0=means[q][:, c0:c1],
+                        scalar=cols[:, TILES + q // 2 : TILES + q // 2 + 1],
+                        in1=gd[:, PASS * q + c0 : PASS * q + c1], op0=ALU.mult, op1=ALU.mult,
+                    )
+                if x == 0 and len(groups[i]) == PACK:
+                    add_base(nc.gpsimd, i, 0, 1)
 
-        def add_base(i):
-            first, width = PASS * halves(i)[0], PASS * len(halves(i))
-            ys[i] = rotating("y", [P, L], F32, 4)
-            nc.vector.tensor_tensor(
-                out=ys[i][:, 0:width], in0=scaled[i][:, 0:width], in1=bs[:, first : first + width], op=ALU.add
-            )
-            for x, q in enumerate(halves(i)):
-                j, lh = divmod(q, 2)
+        def add_base(engine, i, x0, x1):
+            first = PASS * groups[i][x0]
+            for c0, c1 in pieces(groups[i][x0], PASS * (x1 - x0)):
+                part = ys[i][:, PASS * x0 + c0 : PASS * x0 + c1]
+                engine.tensor_tensor(out=part, in0=part, in1=bs[:, first + c0 : first + c1], op=ALU.add)
+            for x in range(x0, x1):
+                j, lh = divmod(groups[i][x], 2)
                 nc.sync.dma_start(
                     out=out_0[P * j : P * (j + 1), PASS * lh : PASS * (lh + 1)], in_=ys[i][:, PASS * x : PASS * (x + 1)]
                 )
 
-        def round_y(i):
-            width = PASS * len(halves(i))
-            y_bf[i] = rotating("y_bf", [P, L], BF16, 2)
-            nc.scalar.copy(
-                out=y_bf[i][:, 0:width].rearrange("n (x u p e) -> n x u p e", u=2, p=P, e=2),
-                in_=ys[i][:, 0:width].rearrange("n (x p u e) -> n x u p e", u=2, p=P, e=2),
-            )
-
-        def turn_y(i):
-            turned[i] = bank(RING_TURN, i)
-            for b in range(2 * len(halves(i))):
-                nc.tensor.transpose(
-                    turned[i][:, P * b : P * (b + 1)], y_bf[i][:].bitcast(F32)[:, P * b : P * (b + 1)], ident[:]
+        def round_y(i, x0, x1):
+            if (i, x0 // 2) not in y_bf:
+                y_bf[i, x0 // 2] = rotating("y_bf", [P, L], BF16, 3)
+            for p0, p1 in pieces(groups[i][x0], P):
+                copy_on(
+                    "vector" if i == len(groups) - 1 else "scalar",
+                    y_bf[i, x0 // 2][:, PASS * (x0 % 2) : PASS * (x0 % 2 + x1 - x0)].rearrange(
+                        "n (x u p e) -> n x u p e", u=2, p=P, e=2)[:, :, :, p0:p1],
+                    ys[i][:, PASS * x0 : PASS * x1].rearrange("n (x p u e) -> n x u p e", u=2, p=P, e=2)[:, :, :, p0:p1],
                 )
 
-        def y_copy(i):
-            words = 2 * P * len(halves(i))
-            y_woven[i] = rotating("y_woven", [P, L], BF16, 2)
+        def turn_y(key, xs):
+            acc = bank(RING_A, len(turned))
+            turned[key, xs] = acc
+            for b in range(2 * xs[0], 2 * xs[1]):
+                nc.tensor.transpose(acc[:, P * b : P * (b + 1)], y_bf[key][:].bitcast(F32)[:, P * b : P * (b + 1)], ident[:])
+            if key not in y_woven:
+                y_woven[key] = rotating("y_woven", [P, L], BF16, 3)
+            w0, w1 = 2 * P * xs[0], 2 * P * xs[1]
             nc.scalar.copy(
-                out=y_woven[i][:].bitcast(F32)[:, 0:words].rearrange("p (x n u) -> p x n u", n=P, u=2),
-                in_=turned[i][:, 0:words].rearrange("p (x u n) -> p x n u", n=P, u=2),
+                out=y_woven[key][:].bitcast(F32)[:, w0:w1].rearrange("p (x n u) -> p x n u", n=P, u=2),
+                in_=acc[:, w0:w1].rearrange("p (x u n) -> p x n u", n=P, u=2),
             )
 
-        def y_quantize(i):
-            for x, q in enumerate(halves(i)):
+        def y_quantize(key, xs=(0, 2)):
+            i, pair = key
+            for x in range(xs[0], xs[1]):
+                q = groups[i][2 * pair + x]
                 j, lh = divmod(q, 2)
                 words = y_words[lh, j // WORD_TILES]
                 at = P * (j % WORD_TILES)
-                quantize(words[:, at : at + P], y_scales[:, lh, P * j : P * (j + 1)], y_woven[i][:, PASS * x : PASS * (x + 1)])
+                quantize(
+                    words[:, at : at + P], y_scales[j // EARLY][:, lh, P * (j % EARLY) : P * (j % EARLY + 1)],
+                    y_woven[key][:, PASS * x : PASS * (x + 1)],
+                )
                 if j % WORD_TILES == WORD_TILES - 1:
                     first = P * (j + 1 - WORD_TILES)
                     nc.sync.dma_start(
                         out=out_1[lh].rearrange("p m t -> p (m t)")[:, PACK * first : PACK * P * (j + 1)].bitcast(I32),
                         in_=words[:].bitcast(I32),
                     )
+                if q == 2 * EARLY - 1:
+                    store_scales(0, [nc.sync])
+                if q == final:
+                    store_scales(1, [nc.sync, nc.scalar])
 
-        steps = TILES + 1
-        for i in range(steps + 3):
-            if i < steps:
-                apply_guide(i)
-            if i == 0:
-                a_weave(len(units) - 1, LAST_SCALAR)
-            if i + AHEAD - 1 < TILES:
-                t_woven[i + AHEAD - 1] = t_copy(t_banks[i + AHEAD - 1])
-            if i + AHEAD - 2 < TILES:
-                t_quantize(i + AHEAD - 2, t_woven[i + AHEAD - 2])
-            if i == 0:
-                a_quantize(len(units) - 1)
-            if 3 <= i < steps + 3:
-                y_quantize(i - 3)
-            if 2 <= i < steps + 2:
-                turn_y(i - 2)
-            if 2 <= i < steps + 2:
-                y_copy(i - 2)
-            if i < steps:
-                add_base(i)
-            if i + AHEAD < TILES:
-                t_banks[i + AHEAD] = t_matmuls(i + AHEAD)
-            for q in reversed(halves(i + 1)):
-                means[q] = mean_matmuls(q)
-            if 1 <= i <= steps:
-                round_y(i - 1)
+        def store_scales(part, queues):
+            m0, m1 = (0, EARLY * P) if part == 0 else (EARLY * P, N)
+            for q in range(4):
+                queues[q % len(queues)].dma_start(
+                    out=out_2[:, 4 * q : 4 * q + 4, m0:m1].rearrange("g r m -> r g m").bitcast(I32),
+                    in_=y_scales[part][32 * q : 32 * q + 4].bitcast(I32),
+                )
 
-        for q in range(4):
-            (nc.scalar if q % 2 else nc.sync).dma_start(
-                out=out_2[:, 4 * q : 4 * q + 4, :].rearrange("g r m -> r g m").bitcast(I32),
-                in_=y_scales[32 * q : 32 * q + 4].bitcast(I32),
-            )
+        def t_tile(j):
+            t_banks[j] = t_matmuls(j)
+            t_woven[j] = t_copy(t_banks[j])
+
+        a_weave_rest(2)
+        t_quantize(1, t_woven[1])
+        a_quantize(2)
+        group_means(0)
+        for j in range(T_EARLY, 3):
+            t_tile(j)
+        ratios(4)
+        apply_guide(0)
+        a_weave_rest(3)
+        t_quantize(2, t_woven[2])
+        a_quantize(3)
+        add_base(nc.vector, 0, 0, 1)
+        add_base(nc.vector, 0, 1, 2)
+        t_tile(3)
+        group_means(1)
+        t_tile(4)
+        round_y(0, 0, 2)
+        turn_y((0, 0), (0, 2))
+        for i in (1, 2, 3):
+            apply_guide(i)
+            fresh = [j for j in (2 * i + 1, 2 * i + 2) if j < TILES]
+            t_quantize(fresh[0], t_woven[fresh[0]])
+            add_base(nc.vector, i, 1, 2)
+            add_base(nc.vector, i, 2, PACK)
+            for j in fresh[1:]:
+                t_quantize(j, t_woven[j])
+            for pair in range(len(groups[i - 1]) // 2):
+                y_quantize((i - 1, pair))
+            group_means(i + 1)
+            for j in fresh:
+                if j + 2 < TILES:
+                    t_tile(j + 2)
+            for pair in range(2):
+                round_y(i, 2 * pair, 2 * pair + 2)
+                turn_y((i, pair), (0, 2))
+        apply_guide(4)
+        add_base(nc.vector, 4, 0, 1)
+        add_base(nc.vector, 4, 1, 2)
+        round_y(4, 0, 1)
+        round_y(4, 1, 2)
+        turn_y((4, 0), (0, 2))
+        y_quantize((3, 0))
+        y_quantize((3, 1))
+        y_quantize((4, 0))

@@ -20,32 +20,23 @@ ENG = mybir.EngineType
 P = 128
 PACK = 4
 PASS = P * PACK
-GROUPS = N // PASS
+RUN = 4
+HALVES = 2
 TILES = N // P
-PIECE = 128
-SCALAR_PIECES = (0, 3, 3)
+PIECES = HALVES * TILES
+SCALE_ROWS = 4
+
 HEAD_SCALAR = 192
-LAST_SCALAR = 128
-T0_ENG = ("scalar", "scalar")
-T_FIRST = 10
-GP_WEAVE = (192, 192, 192, 128)
-SCALAR_SHARE = 3
+A_GPSIMD = 192
+A_GPSIMD_LAST = 128
+BLEND_SCALAR_SLOT = 4
+T_SLOT = 10
 T_EARLY = 3
-SQ_FIRST = 4
-A_FIRST = 8
-A_STEP = 3
-A_SCALAR = 0
-SORT_AT = 1
-LAG = 2
-GP_ADD = 384
-GP_FROM = 1
-GP_TO = 1
-EARLY = 4
-AHEAD = 4
-BL_FIRST = 3
-BL_STEP = 3
+
 WORD_TILES = 2
-RING_A, RING_B, RING_T = (0, 1), (2, 3, 4, 5), (6, 7)
+EARLY_TILES = 4
+
+DEN_BANKS, NUM_BANKS, T_BANKS = (0, 1), (2, 3, 4, 5), (6, 7)
 
 
 def tile_mean_free_guided_pass_k4_kernel(
@@ -65,95 +56,90 @@ def tile_mean_free_guided_pass_k4_kernel(
         def rotating(tag, shape, dtype, bufs):
             return work.tile(shape, dtype, name=tag, tag=tag, bufs=bufs, align_bytes=64)
 
-        def bank(ring, count):
-            name = "bank%d" % ring[count % len(ring)]
+        def bank(banks, count):
+            name = "bank%d" % banks[count % len(banks)]
             return psum.tile([P, PASS], F32, name=name, tag=name)
 
-        v_words = [kept("v_words%d" % h, [P, GROUPS, N], U8) for h in range(2)]
-        v_scales = kept("v_scales", [P, GROUPS, N], U8)
-        vp_words = [kept("vp_words%d" % h, [P, GROUPS, N], U8) for h in range(2)]
-        vp_scales = kept("vp_scales", [P, GROUPS, N], U8)
-        c_scales = kept("c_scales", [P, GROUPS, L], U8)
-        c_words = [kept("c_words%d" % lh, [P, GROUPS, PASS], U32) for lh in range(2)]
-        sq_raw = {(g, lh): kept("sq_raw%d%d" % (g, lh), [P, PACK, PASS], BF16) for g in range(2) for lh in range(2)}
-        bl_raw = [kept("bl_raw%d" % g, [P, PACK, N], BF16) for g in range(2)]
-        gd = kept("guide", [P, TILES * L], BF16)
-        bs = kept("base", [P, TILES * L], BF16)
-        pairs = [(a, b) for a in range(2) for b in range(2)]
-        sq_q = {k: (kept("sq_c%d%d" % k, [P, PASS], U32), kept("sq_s%d%d" % k, [P, PASS], U8)) for k in pairs}
-        bl_q = {k: (kept("bl_c%d%d" % k, [P, PASS], U32), kept("bl_s%d%d" % k, [P, PASS], U8)) for k in pairs}
-        a_q = {k: (kept("a_c%d%d" % k, [P, PASS], U32), kept("a_s%d%d" % k, [P, PASS], U8)) for k in pairs}
-        t_q = [(kept("t_c%d" % j, [P, 2 * P], U32), kept("t_s%d" % j, [P, 2 * P], U8)) for j in range(TILES)]
-        y_words = {
-            (lh, i): kept("y_words%d%d" % (lh, i), [P, WORD_TILES * P], U32)
-            for lh in range(2) for i in range(TILES // WORD_TILES)
-        }
-        y_scales = [kept("y_scales0", [P, 2, EARLY * P], U8), kept("y_scales1", [P, 2, N - EARLY * P], U8)]
-        rows = kept("rows", [P, 3 * P], BF16)
-        ident = kept("ident", [P, P], F32)
-        ident_bf = kept("ident_bf", [P, TILES], BF16)
-        cols = kept("cols", [P, 2 * TILES], F32)
+        def quantised(name, key, width):
+            return kept("%s_codes%s" % (name, key), [P, width], U32), kept("%s_scales%s" % (name, key), [P, width], U8)
 
-        warm = kept("warm", [P, 2], F32)
+        halves = range(HALVES)
+        pairs = [(a, b) for a in halves for b in halves]
+        v_words = [kept("v_words%d" % h, [P, HALVES, N], U8) for h in halves]
+        v_scales = kept("v_scales", [P, HALVES, N], U8)
+        v_words_sorted = [kept("v_words_sorted%d" % h, [P, HALVES, N], U8) for h in halves]
+        v_scales_sorted = kept("v_scales_sorted", [P, HALVES, N], U8)
+        c_scales = kept("c_scales", [P, HALVES, L], U8)
+        c_words = [kept("c_words%d" % lh, [P, HALVES, PASS], U32) for lh in halves]
+        square_rows = {(g, lh): kept("square_rows%d%d" % (g, lh), [P, PACK, PASS], BF16) for g, lh in pairs}
+        blend_rows = [kept("blend_rows%d" % g, [P, PACK, N], BF16) for g in halves]
+        guide_sb = kept("guide_sb", [P, TILES * L], BF16)
+        base_sb = kept("base_sb", [P, TILES * L], BF16)
+        square_q = {(g, lh): quantised("square", "%d%d" % (g, lh), PASS) for g, lh in pairs}
+        blend_q = {(g, h): quantised("blend", "%d%d" % (g, h), PASS) for g, h in pairs}
+        a_q = {(h, lh): quantised("a", "%d%d" % (h, lh), PASS) for h, lh in pairs}
+        t_q = [quantised("t", "%d" % j, HALVES * P) for j in range(TILES)]
+        y_words = [kept("y_words%d" % i, [P, HALVES, WORD_TILES * P], U32) for i in range(TILES // WORD_TILES)]
+        y_scales = [kept("y_scales%d" % part, [P, HALVES, EARLY_TILES * P], U8) for part in range(TILES // EARLY_TILES)]
+        line_rows = kept("line_rows", [P, PASS + P], BF16)
+        conf_sorted = kept("conf_sorted", [P, PASS], BF16)
+        identity = kept("identity", [P, P], F32)
+        identity_bf = kept("identity_bf", [P, TILES], BF16)
+        line_cols = kept("line_cols", [P, 2 * TILES], F32)
 
-        make_identity(nc, ident[:])
-        nc.gpsimd.tensor_copy(out=ident_bf[:], in_=ident[:, 0:TILES])
-        nc.gpsimd.memset(rows[:], 0.0)
+        nc.gpsimd.memset(line_rows[:], 0.0)
+        nc.scalar.dma_start(out=line_rows[0:HALVES, 0:PASS], in_=conf.rearrange("(h c) -> h c", h=HALVES))
+        nc.scalar.dma_start(out=line_rows[0:TILES, PASS:], in_=norm.rearrange("(j p) -> j p", p=P))
+        make_identity(nc, identity[:])
+        nc.gpsimd.tensor_copy(out=identity_bf[:], in_=identity[:, 0:TILES])
         nc.vector.memset(v_scales[:].rearrange("p g n -> p (g n)").bitcast(I32), 0)
         nc.vector.memset(c_scales[:].rearrange("p g n -> p (g n)").bitcast(I32), 0)
 
+        def quadrant(plane, quad):
+            return plane[32 * quad : 32 * quad + SCALE_ROWS].bitcast(I32)
+
+        def scale_rows(dram, quad):
+            return dram[:, SCALE_ROWS * quad : SCALE_ROWS * (quad + 1), :].rearrange("g r n -> r g n").bitcast(I32)
+
         def load_scales(plane, dram):
-            for q in range(4):
-                nc.sync.dma_start(
-                    out=plane[32 * q : 32 * q + 4].bitcast(I32),
-                    in_=dram[:, 4 * q : 4 * q + 4, :].rearrange("g r n -> r g n").bitcast(I32),
-                )
+            for quad in range(P // 32):
+                nc.sync.dma_start(out=quadrant(plane, quad), in_=scale_rows(dram, quad))
 
-        def load_rows(raw, dram, g, half):
-            nc.sync.dma_start(
-                out=raw[g, half][:],
-                in_=dram[PASS * g : PASS * (g + 1), PASS * half : PASS * (half + 1)].rearrange("(p j) l -> p j l", j=PACK),
-            )
+        def by_word(rows):
+            return rows.rearrange("(p j) x -> p j x", j=PACK)
 
-        def load_cross(lh):
-            nc.sync.dma_start(
-                out=c_words[lh][:].bitcast(I32),
-                in_=cross_words.rearrange("g p l t -> p g (l t)")[:, :, PACK * PASS * lh : PACK * PASS * (lh + 1)].bitcast(I32),
-            )
-
-        def load_window(h):
-            nc.sync.dma_start(
-                out=v_words[h][:].bitcast(I32),
-                in_=win_words.rearrange("g p b -> p g b")[:, :, N * h : N * (h + 1)].bitcast(I32),
-            )
+        def load_square(g, lh):
+            rows = square[PASS * g : PASS * (g + 1), PASS * lh : PASS * (lh + 1)]
+            nc.sync.dma_start(out=square_rows[g, lh][:], in_=by_word(rows))
 
         def load_blend(g):
-            nc.sync.dma_start(
-                out=bl_raw[g][:], in_=blend[PASS * g : PASS * (g + 1), :].rearrange("(p j) c -> p j c", j=PACK)
-            )
+            nc.sync.dma_start(out=blend_rows[g][:], in_=by_word(blend[PASS * g : PASS * (g + 1), :]))
 
-        load_rows(sq_raw, square, 0, 0)
-        load_rows(sq_raw, square, 1, 0)
+        def load_window(h):
+            columns = win_words.rearrange("g p b -> p g b")[:, :, N * h : N * (h + 1)]
+            nc.sync.dma_start(out=v_words[h][:].bitcast(I32), in_=columns.bitcast(I32))
+
+        def load_cross(lh):
+            columns = cross_words.rearrange("g p l t -> p g (l t)")[:, :, PACK * PASS * lh : PACK * PASS * (lh + 1)]
+            nc.sync.dma_start(out=c_words[lh][:].bitcast(I32), in_=columns.bitcast(I32))
+
+        load_square(0, 0)
+        load_square(1, 0)
         load_window(0)
         load_scales(v_scales, win_scales)
-        load_rows(sq_raw, square, 0, 1)
-        nc.sync.dma_start(
-            out=rows[0:PACK, 0 : 2 * P].rearrange("t (m r) -> t m r", r=4),
-            in_=conf.rearrange("(m t r) -> t m r", t=PACK, r=4),
-        )
-        nc.sync.dma_start(out=rows[0:TILES, 2 * P : 3 * P], in_=norm.rearrange("(j p) -> j p", p=P))
+        load_square(0, 1)
         load_scales(c_scales, cross_scales)
         load_cross(0)
         load_window(1)
-        load_rows(sq_raw, square, 1, 1)
+        load_square(1, 1)
         load_blend(1)
         load_blend(0)
         load_cross(1)
         for i in range(TILES // 2):
-            for dst, src in ((gd, guide), (bs, base)):
+            for tile_sb, dram in ((guide_sb, guide), (base_sb, base)):
                 nc.sync.dma_start(
-                    out=dst[:, 2 * L * i : 2 * L * (i + 1)].rearrange("p (j l) -> p j l", j=2),
-                    in_=src[2 * P * i : 2 * P * (i + 1), :].rearrange("(j p) l -> p j l", p=P),
+                    out=tile_sb[:, 2 * L * i : 2 * L * (i + 1)].rearrange("p (j l) -> p j l", j=2),
+                    in_=dram[2 * P * i : 2 * P * (i + 1), :].rearrange("(j p) l -> p j l", p=P),
                 )
 
         def copy_on(engine, out, in_):
@@ -164,362 +150,358 @@ def tile_mean_free_guided_pass_k4_kernel(
             else:
                 nc.vector.tensor_copy(out=out, in_=in_)
 
-        def quantize(dst_codes, dst_scales, src):
-            nc.vector.quantize_mx(out=dst_codes.bitcast(FP8X4), scales=dst_scales, in_=src)
+        def quantize(codes, scales, woven):
+            nc.vector.quantize_mx(out=codes.bitcast(FP8X4), scales=scales, in_=woven)
 
-        def weave_rows(engine, woven, raw, c0, c1):
+        def quantize_tile(tiles, woven):
+            quantize(tiles[0][:], tiles[1][:], woven[:])
+
+        def weave(engine, woven, rows, c0, c1):
             copy_on(
                 engine,
-                woven[:, PACK * c0 : PACK * c1].rearrange("p (c i j) -> p c j i", i=4, j=PACK),
-                raw[:, :, c0:c1].rearrange("p j (c i) -> p c j i", i=4),
+                woven[:, PACK * c0 : PACK * c1].rearrange("p (c j) -> p c j", j=PACK),
+                rows[:, :, c0:c1].rearrange("p j c -> p c j"),
             )
 
-        def weave_blend(engine, woven, raw, c0, c1):
-            slots_here = slice(c0 // P, c1 // P)
+        def weave_blend(engine, woven, g, h, t0, t1):
+            rows = blend_rows[g][:, :, PASS * h : PASS * (h + 1)]
             copy_on(
                 engine,
-                woven[:].rearrange("p (t m r j) -> p m t j r", t=PACK, r=4, j=PACK)[:, :, slots_here],
-                raw.rearrange("p j (m t r) -> p m t j r", t=PACK, r=4)[:, :, slots_here],
+                woven[:].rearrange("p (t m r j) -> p t m r j", t=PACK, r=RUN, j=PACK)[:, t0:t1],
+                rows.rearrange("p j (m t r) -> p t m r j", t=PACK, r=RUN)[:, t0:t1],
             )
 
         def new_woven():
             return rotating("woven", [P, PACK * PASS], BF16, 5)
 
-        nc.vector.memset(warm[:, 0:1], 1.0)
-        nc.scalar.activation(out=warm[:, 1:2], in_=warm[:, 0:1], func=ACT.Abs_reciprocal_sqrt)
-        head = [new_woven(), new_woven()]
+        def woven_square(g, lh):
+            woven = new_woven()
+            weave("vector", woven, square_rows[g, lh], 0, PASS)
+            return woven
+
+        def woven_blend(g, h):
+            woven = new_woven()
+            weave_blend("vector", woven, g, h, 0, PACK)
+            return woven
+
         def sort_window(h):
             nc.vector.tensor_copy(
-                out=vp_words[h][:].bitcast(I32).rearrange("p g (t m w) -> p g t m w", t=PACK, w=2),
+                out=v_words_sorted[h][:].bitcast(I32).rearrange("p g (t m w) -> p g t m w", t=PACK, w=2),
                 in_=v_words[h][:].bitcast(I32).rearrange("p g (m t w) -> p g t m w", t=PACK, w=2),
             )
 
-        weave_rows("scalar", head[0], sq_raw[0, 0], 0, HEAD_SCALAR)
-        weave_rows("vector", head[0], sq_raw[0, 0], HEAD_SCALAR, PASS)
-        nc.vector.tensor_copy(
-            out=vp_scales[:].bitcast(I32).rearrange("p g (h t m) -> p (g h) t m", h=2, t=PACK),
-            in_=v_scales[:].bitcast(I32).rearrange("p g (h m t) -> p (g h) t m", h=2, t=PACK),
-        )
-        quantize(sq_q[0, 0][0][:], sq_q[0, 0][1][:], head[0][:])
-        weave_rows("scalar", head[1], sq_raw[1, 0], 0, HEAD_SCALAR)
-        weave_rows("vector", head[1], sq_raw[1, 0], HEAD_SCALAR, PASS)
+        def sort_window_scales():
+            nc.vector.tensor_copy(
+                out=v_scales_sorted[:].bitcast(I32).rearrange("p g (h t m) -> p (g h) t m", h=HALVES, t=PACK),
+                in_=v_scales[:].bitcast(I32).rearrange("p g (h m t) -> p (g h) t m", h=HALVES, t=PACK),
+            )
+
+        head = [new_woven() for g in halves]
+        weave("scalar", head[0], square_rows[0, 0], 0, HEAD_SCALAR)
+        weave("vector", head[0], square_rows[0, 0], HEAD_SCALAR, PASS)
+        sort_window_scales()
+        quantize_tile(square_q[0, 0], head[0])
+        weave("scalar", head[1], square_rows[1, 0], 0, HEAD_SCALAR)
+        weave("vector", head[1], square_rows[1, 0], HEAD_SCALAR, PASS)
         sort_window(0)
-        quantize(sq_q[1, 0][0][:], sq_q[1, 0][1][:], head[1][:])
+        quantize_tile(square_q[1, 0], head[1])
 
         def line_columns():
-            col_bank = bank(RING_T, 1)
-            for h in range(2):
-                nc.tensor.matmul(
-                    col_bank[:, PACK * h : PACK * (h + 1)], lhsT=rows[:, P * h : P * (h + 1)], rhs=ident_bf[:, 0:PACK],
-                    start=True, stop=True,
-                )
-            nc.tensor.matmul(
-                col_bank[:, TILES : 2 * TILES], lhsT=rows[:, 2 * P : 3 * P], rhs=ident_bf[:], start=True, stop=True
+            nc.scalar.copy(
+                out=conf_sorted[:].rearrange("h (t m r) -> h t m r", t=PACK, r=RUN),
+                in_=line_rows[:, 0:PASS].rearrange("h (m t r) -> h t m r", t=PACK, r=RUN),
             )
-            nc.scalar.copy(out=cols[:], in_=col_bank[:, 0 : 2 * TILES])
+            turned_lines = bank(T_BANKS, 1)
+            blocks = [(conf_sorted[:, P * t : P * (t + 1)], HALVES * t, HALVES) for t in range(PACK)]
+            for rows, first, count in blocks + [(line_rows[:, PASS:], TILES, TILES)]:
+                nc.tensor.matmul(
+                    turned_lines[:, first : first + count], lhsT=rows, rhs=identity_bf[:, 0:count], start=True, stop=True
+                )
+            nc.scalar.copy(out=line_cols[:], in_=turned_lines[:, 0 : 2 * TILES])
 
-        def moment(s, operand, ring):
-            (h, lh), t = units[slots[s][0]], slots[s][1]
-            slot = PACK * h + t
-            acc = bank(ring, s)
-            for g in range(GROUPS):
+        units = [(h, lh) for lh in halves for h in halves]
+        slots = len(units) * PACK
+        root, recip, nums, a_rows, a_woven, t_sums, t_woven = {}, {}, {}, {}, {}, {}, {}
+
+        def moment(s, operand, banks):
+            (h, lh), t = units[s // PACK], s % PACK
+            acc = bank(banks, s)
+            for g in halves:
                 codes, scales = operand(g, lh)
                 nc.tensor.matmul_mx(
                     out=acc[:],
-                    lhsT=vp_words[h][:, g, 2 * P * t : 2 * P * (t + 1)].bitcast(FP4X4),
-                    lhsT_scale=vp_scales[:, g, P * slot : P * (slot + 1)],
+                    lhsT=v_words_sorted[h][:, g, 2 * P * t : 2 * P * (t + 1)].bitcast(FP4X4),
+                    lhsT_scale=v_scales_sorted[:, g, PASS * h + P * t : PASS * h + P * (t + 1)],
                     rhs=codes.bitcast(FP8X4), rhs_scale=scales,
-                    start=(g == 0), stop=(g == GROUPS - 1),
+                    start=(g == 0), stop=(g == HALVES - 1),
                 )
             return acc
 
         def square_operand(g, lh):
-            return sq_q[g, lh][0][:], sq_q[g, lh][1][:]
+            return square_q[g, lh][0][:], square_q[g, lh][1][:]
 
         def cross_operand(g, lh):
             return c_words[lh][:, g, :], c_scales[:, g, PASS * lh : PASS * (lh + 1)]
 
-        def t_matmuls(j):
-            banks = [bank(RING_T, 2 * j + h) for h in range(2)]
-            for h in range(2):
-                for t in range(PACK):
-                    for g in range(GROUPS):
-                        nc.tensor.matmul_mx(
-                            out=banks[h][:, P * t : P * (t + 1)],
-                            lhsT=bl_q[g, h][0][:, P * t : P * (t + 1)].bitcast(FP8X4),
-                            lhsT_scale=bl_q[g, h][1][:, P * t : P * (t + 1)],
-                            rhs=v_words[j // PACK][:, g, 2 * P * (j % PACK) : 2 * P * (j % PACK + 1)].bitcast(FP4X4),
-                            rhs_scale=v_scales[:, g, P * j : P * (j + 1)],
-                            start=(g == 0), stop=(g == GROUPS - 1),
-                        )
-            return banks
+        def inverse_root(s, den):
+            root[s] = rotating("root", [P, PASS], F32, 2)
+            nc.scalar.activation(out=root[s][:], in_=den[:], func=ACT.Abs_reciprocal_sqrt)
 
-        def t_copy(banks, engines=("scalar", "scalar")):
-            woven = rotating("t_woven", [P, 2 * PASS], BF16, 3)
-            for h in range(2):
-                copy_on(
-                    engines[h],
-                    woven[:, PASS * h : PASS * (h + 1)].rearrange("p (n t) -> p n t", t=PACK),
-                    banks[h][:].rearrange("p (t n) -> p n t", t=PACK),
-                )
-            return woven
-
-        def t_quantize(j, woven):
-            quantize(t_q[j][0][:], t_q[j][1][:], woven[:])
-
-        def mean_matmuls(q, count):
-            j, lh = divmod(q, 2)
-            acc = bank(RING_B, count)
-            for h in range(2):
-                nc.tensor.matmul_mx(
-                    out=acc[:],
-                    lhsT=t_q[j][0][:, P * h : P * (h + 1)].bitcast(FP8X4),
-                    lhsT_scale=t_q[j][1][:, P * h : P * (h + 1)],
-                    rhs=a_q[h, lh][0][:].bitcast(FP8X4), rhs_scale=a_q[h, lh][1][:],
-                    start=(h == 0), stop=(h == 1),
-                )
-            return acc
-
-        units = [(h, lh) for lh in range(2) for h in range(2)]
-        slots = [(u, t) for u in range(len(units)) for t in range(PACK)]
-        later = [
-            (lambda e, w, g, c0, c1: weave_rows(e, w, sq_raw[g, 1], c0, c1), lambda g: sq_q[g, 1]),
-            (lambda e, w, g, c0, c1: weave_blend(e, w, bl_raw[g][:, :, 0:PASS], c0, c1), lambda g: bl_q[g, 0]),
-            (lambda e, w, g, c0, c1: weave_blend(e, w, bl_raw[g][:, :, PASS:N], c0, c1), lambda g: bl_q[g, 1]),
-        ]
-        root, recip, nums, a_rows, a_woven, prep, t_banks, t_woven = {}, {}, {}, {}, {}, {}, {}, {}
-
-        def square_root_step(s):
-            recip[s] = rotating("recip", [P, PASS], F32, 5)
+        def reciprocal(s):
+            recip[s] = rotating("recip", [P, PASS], F32, PACK + 1)
             nc.scalar.activation(out=recip[s][:], in_=root[s][:], func=ACT.Square)
 
         def ratio(s):
-            u, t = slots[s]
+            u, t = divmod(s, PACK)
             if t == 0:
                 a_rows[u] = rotating("a_rows", [P, PACK, PASS], BF16, 2)
-            slot = PACK * units[u][0] + t
+            column = HALVES * t + units[u][0]
             nc.vector.scalar_tensor_tensor(
-                out=a_rows[u][:, t, :], in0=nums[s][:], scalar=cols[:, slot : slot + 1], in1=recip[s][:],
+                out=a_rows[u][:, t, :], in0=nums[s][:], scalar=line_cols[:, column : column + 1], in1=recip[s][:],
                 op0=ALU.mult, op1=ALU.mult,
             )
 
-        def a_weave_first(u):
-            a_woven[u] = rotating("a_woven", [P, PACK * PASS], BF16, 2)
-            weave_rows("gpsimd", a_woven[u], a_rows[u], 0, GP_WEAVE[u])
+        def gpsimd_share(u):
+            return A_GPSIMD_LAST if u == len(units) - 1 else A_GPSIMD
 
-        def a_weave_rest(u):
-            weave_rows("vector", a_woven[u], a_rows[u], GP_WEAVE[u], PASS)
-
-        def a_quantize(u):
-            quantize(a_q[units[u]][0][:], a_q[units[u]][1][:], a_woven[u][:])
-
-        def prep_quantize(u, g):
-            codes, scales = later[u][1](g)
-            quantize(codes[:], scales[:], prep[u, g][:])
-
-        def prep_weave(b, g):
-            prep[b, g] = new_woven()
-            later[b][0]("vector", prep[b, g], g, 0, PASS)
-
-        def t_step(s):
-            j, odd = divmod(s - T_FIRST, 2)
-            if 0 <= j < T_EARLY and odd:
-                t_woven[j] = t_copy(t_banks[j])
-            if 0 <= j < T_EARLY and not odd:
-                t_banks[j] = t_matmuls(j)
-
-        def between(b):
-            if b == 0:
-                prep_weave(0, 0)
-                sort_window(1)
-                prep_quantize(0, 0)
-            if b == 1:
-                prep_weave(0, 1)
-                prep_weave(1, 1)
-                prep_quantize(0, 1)
-                prep_weave(2, 1)
-                prep_quantize(1, 1)
-                prep_quantize(2, 1)
-            if b == 2:
-                prep_weave(1, 0)
-                if SCALAR_SHARE < PACK:
-                    later[2][0]("vector", prep[2, 0], 0, PIECE * SCALAR_SHARE, PASS)
-                a_weave_rest(0)
-                prep_quantize(1, 0)
-                prep_quantize(2, 0)
-                a_quantize(0)
-            if b == 3:
-                a_weave_rest(1)
-                t_quantize(0, t_woven[0])
-                a_quantize(1)
-
-        def ratios(b):
-            run = [s for s in range(PACK * b - 1, PACK * b + PACK - 1) if 0 <= s < len(slots)]
-            for s in run:
+        def ratio_run(b):
+            for s in range(max(PACK * b - 1, 0), min(PACK * (b + 1) - 1, slots)):
                 ratio(s)
                 if s % PACK == PACK - 1:
-                    a_weave_first(s // PACK)
+                    u = s // PACK
+                    a_woven[u] = rotating("a_woven", [P, PACK * PASS], BF16, 2)
+                    weave("gpsimd", a_woven[u], a_rows[u], 0, gpsimd_share(u))
 
-        between(0)
-        for s in range(len(slots)):
+        def a_weave_rest(u):
+            weave("vector", a_woven[u], a_rows[u], gpsimd_share(u), PASS)
+
+        def t_matmuls(j):
+            t_sums[j] = [bank(T_BANKS, h) for h in halves]
+            window = v_words[j // PACK]
+            for h in halves:
+                for t in range(PACK):
+                    for g in halves:
+                        nc.tensor.matmul_mx(
+                            out=t_sums[j][h][:, P * t : P * (t + 1)],
+                            lhsT=blend_q[g, h][0][:, P * t : P * (t + 1)].bitcast(FP8X4),
+                            lhsT_scale=blend_q[g, h][1][:, P * t : P * (t + 1)],
+                            rhs=window[:, g, 2 * P * (j % PACK) : 2 * P * (j % PACK + 1)].bitcast(FP4X4),
+                            rhs_scale=v_scales[:, g, P * j : P * (j + 1)],
+                            start=(g == 0), stop=(g == HALVES - 1),
+                        )
+
+        def t_copy(j):
+            t_woven[j] = rotating("t_woven", [P, HALVES * PASS], BF16, T_EARLY)
+            for h in halves:
+                nc.scalar.copy(
+                    out=t_woven[j][:, PASS * h : PASS * (h + 1)].rearrange("p (n t) -> p n t", t=PACK),
+                    in_=t_sums[j][h][:].rearrange("p (t n) -> p n t", t=PACK),
+                )
+
+        def t_quantize(j):
+            quantize_tile(t_q[j], t_woven[j])
+
+        def finish_unit(u, j):
+            a_weave_rest(u)
+            t_quantize(j)
+            quantize_tile(a_q[units[u]], a_woven[u])
+
+        def before_run_0():
+            woven = woven_square(0, 1)
+            sort_window(1)
+            quantize_tile(square_q[0, 1], woven)
+
+        def before_run_1():
+            last_square = woven_square(1, 1)
+            first_blend = woven_blend(1, 0)
+            quantize_tile(square_q[1, 1], last_square)
+            second_blend = woven_blend(1, 1)
+            quantize_tile(blend_q[1, 0], first_blend)
+            quantize_tile(blend_q[1, 1], second_blend)
+
+        def before_run_2(last_blend):
+            third_blend = woven_blend(0, 0)
+            a_weave_rest(0)
+            quantize_tile(blend_q[0, 0], third_blend)
+            quantize_tile(blend_q[0, 1], last_blend)
+            quantize_tile(a_q[units[0]], a_woven[0])
+
+        line_columns()
+        before_run_0()
+        for s in range(slots):
             b, t = divmod(s, PACK)
-            den = moment(s, square_operand, RING_A)
+            den = moment(s, square_operand, DEN_BANKS)
             if t < PACK - 1:
-                nums[s] = moment(s, cross_operand, RING_B)
-            root[s] = rotating("root", [P, PASS], F32, 2)
-            nc.scalar.activation(out=root[s][:], in_=den[:], func=ACT.Abs_reciprocal_sqrt)
-            if s == 0:
-                line_columns()
+                nums[s] = moment(s, cross_operand, NUM_BANKS)
+            inverse_root(s, den)
             if s > 0:
-                square_root_step(s - 1)
-            at = s - SQ_FIRST
-            if at == 0:
-                prep[2, 0] = new_woven()
-            if 0 <= at < SCALAR_SHARE:
-                later[2][0]("scalar", prep[2, 0], 0, PIECE * at, PIECE * (at + 1))
-            t_step(s)
+                reciprocal(s - 1)
+            if s == BLEND_SCALAR_SLOT:
+                scalar_blend = new_woven()
+            if 0 <= s - BLEND_SCALAR_SLOT < PACK:
+                weave_blend("scalar", scalar_blend, 0, 1, s - BLEND_SCALAR_SLOT, s - BLEND_SCALAR_SLOT + 1)
+            j, second = divmod(s - T_SLOT, 2)
+            if 0 <= j < T_EARLY:
+                (t_copy if second else t_matmuls)(j)
             if t == PACK - 1:
-                if b == 3:
-                    between(3)
-                ratios(b)
-                nums[s] = moment(s, cross_operand, RING_B)
-                if b < 2:
-                    between(b + 1)
-        square_root_step(len(slots) - 1)
+                if b == len(units) - 1:
+                    finish_unit(1, 0)
+                ratio_run(b)
+                nums[s] = moment(s, cross_operand, NUM_BANKS)
+                if b == 0:
+                    before_run_1()
+                if b == 1:
+                    before_run_2(scalar_blend)
+        reciprocal(slots - 1)
 
-        groups = [[0, 2], [1, 3, 4, 5], [6, 7, 8, 9], [10, 11, 12, 13], [14, 15]]
-        final = 2 * TILES - 1
-        means, ys, y_bf, y_woven, turned = {}, {}, {}, {}, {}
+        first_group, last_group = [0, 2], [PIECES - 2, PIECES - 1]
+        middle = [q for q in range(PIECES) if q not in first_group + last_group]
+        groups = [first_group] + [middle[x : x + PACK] for x in range(0, len(middle), PACK)] + [last_group]
+        last = len(groups) - 1
+        means, ys, y_bf, y_woven = {}, {}, {}, {}
 
-        def pieces(q, width):
-            return [(0, width // 2), (width // 2, width)] if q == final else [(0, width)]
+        def parts(q, width):
+            return [(0, width // 2), (width // 2, width)] if q == PIECES - 1 else [(0, width)]
 
         def group_means(i):
             for q in groups[i]:
-                means[q] = mean_matmuls(q, len(means))
+                j, lh = divmod(q, HALVES)
+                means[q] = bank(NUM_BANKS, len(means))
+                for h in halves:
+                    nc.tensor.matmul_mx(
+                        out=means[q][:],
+                        lhsT=t_q[j][0][:, P * h : P * (h + 1)].bitcast(FP8X4),
+                        lhsT_scale=t_q[j][1][:, P * h : P * (h + 1)],
+                        rhs=a_q[h, lh][0][:].bitcast(FP8X4), rhs_scale=a_q[h, lh][1][:],
+                        start=(h == 0), stop=(h == HALVES - 1),
+                    )
 
         def apply_guide(i):
             ys[i] = rotating("y", [P, PACK * PASS], F32, 3)
             for x, q in enumerate(groups[i]):
-                for c0, c1 in pieces(q, PASS):
+                column = TILES + q // HALVES
+                for c0, c1 in parts(q, PASS):
                     nc.vector.scalar_tensor_tensor(
                         out=ys[i][:, PASS * x + c0 : PASS * x + c1], in0=means[q][:, c0:c1],
-                        scalar=cols[:, TILES + q // 2 : TILES + q // 2 + 1],
-                        in1=gd[:, PASS * q + c0 : PASS * q + c1], op0=ALU.mult, op1=ALU.mult,
+                        scalar=line_cols[:, column : column + 1],
+                        in1=guide_sb[:, PASS * q + c0 : PASS * q + c1], op0=ALU.mult, op1=ALU.mult,
                     )
                 if x == 0 and len(groups[i]) == PACK:
                     add_base(nc.gpsimd, i, 0, 1)
 
         def add_base(engine, i, x0, x1):
             first = PASS * groups[i][x0]
-            for c0, c1 in pieces(groups[i][x0], PASS * (x1 - x0)):
+            for c0, c1 in parts(groups[i][x0], PASS * (x1 - x0)):
                 part = ys[i][:, PASS * x0 + c0 : PASS * x0 + c1]
-                engine.tensor_tensor(out=part, in0=part, in1=bs[:, first + c0 : first + c1], op=ALU.add)
-            for x in range(x0, x1):
-                j, lh = divmod(groups[i][x], 2)
+                engine.tensor_tensor(out=part, in0=part, in1=base_sb[:, first + c0 : first + c1], op=ALU.add)
+
+        def store_y(i, x):
+            tiles = [groups[i][x] // HALVES, groups[i][x + 1] // HALVES]
+            if tiles[0] == tiles[1]:
+                nc.sync.dma_start(out=out_0[P * tiles[0] : P * (tiles[0] + 1), :], in_=ys[i][:, PASS * x : PASS * (x + 2)])
+                return
+            for place, j in enumerate(tiles, start=x):
+                lh = groups[i][place] % HALVES
                 nc.sync.dma_start(
-                    out=out_0[P * j : P * (j + 1), PASS * lh : PASS * (lh + 1)], in_=ys[i][:, PASS * x : PASS * (x + 1)]
+                    out=out_0[P * j : P * (j + 1), PASS * lh : PASS * (lh + 1)],
+                    in_=ys[i][:, PASS * place : PASS * (place + 1)],
                 )
 
-        def round_y(i, x0, x1):
-            if (i, x0 // 2) not in y_bf:
-                y_bf[i, x0 // 2] = rotating("y_bf", [P, L], BF16, 3)
-            for p0, p1 in pieces(groups[i][x0], P):
+        def round_y(engine, i, x0, x1):
+            pair = (i, x0 // 2)
+            if x0 % 2 == 0:
+                y_bf[pair] = rotating("y_bf", [P, 2 * PASS], BF16, 3)
+            rounded = y_bf[pair][:, PASS * (x0 % 2) : PASS * (x0 % 2 + x1 - x0)]
+            for p0, p1 in parts(groups[i][x0], P):
                 copy_on(
-                    "vector" if i == len(groups) - 1 else "scalar",
-                    y_bf[i, x0 // 2][:, PASS * (x0 % 2) : PASS * (x0 % 2 + x1 - x0)].rearrange(
-                        "n (x u p e) -> n x u p e", u=2, p=P, e=2)[:, :, :, p0:p1],
+                    engine,
+                    rounded.rearrange("n (x u p e) -> n x u p e", u=2, p=P, e=2)[:, :, :, p0:p1],
                     ys[i][:, PASS * x0 : PASS * x1].rearrange("n (x p u e) -> n x u p e", u=2, p=P, e=2)[:, :, :, p0:p1],
                 )
 
-        def turn_y(key, xs):
-            acc = bank(RING_A, len(turned))
-            turned[key, xs] = acc
-            for b in range(2 * xs[0], 2 * xs[1]):
-                nc.tensor.transpose(acc[:, P * b : P * (b + 1)], y_bf[key][:].bitcast(F32)[:, P * b : P * (b + 1)], ident[:])
-            if key not in y_woven:
-                y_woven[key] = rotating("y_woven", [P, L], BF16, 3)
-            w0, w1 = 2 * P * xs[0], 2 * P * xs[1]
+        def turn_y(pair):
+            turned = bank(DEN_BANKS, len(y_woven))
+            words = y_bf[pair][:].bitcast(F32)
+            for block in range(PASS // P):
+                nc.tensor.transpose(
+                    turned[:, P * block : P * (block + 1)], words[:, P * block : P * (block + 1)], identity[:]
+                )
+            y_woven[pair] = rotating("y_woven", [P, 2 * PASS], BF16, 3)
             nc.scalar.copy(
-                out=y_woven[key][:].bitcast(F32)[:, w0:w1].rearrange("p (x n u) -> p x n u", n=P, u=2),
-                in_=acc[:, w0:w1].rearrange("p (x u n) -> p x n u", n=P, u=2),
+                out=y_woven[pair][:].bitcast(F32).rearrange("p (x n u) -> p x n u", n=P, u=2),
+                in_=turned[:].rearrange("p (x u n) -> p x n u", n=P, u=2),
             )
 
-        def y_quantize(key, xs=(0, 2)):
-            i, pair = key
-            for x in range(xs[0], xs[1]):
-                q = groups[i][2 * pair + x]
-                j, lh = divmod(q, 2)
-                words = y_words[lh, j // WORD_TILES]
-                at = P * (j % WORD_TILES)
-                quantize(
-                    words[:, at : at + P], y_scales[j // EARLY][:, lh, P * (j % EARLY) : P * (j % EARLY + 1)],
-                    y_woven[key][:, PASS * x : PASS * (x + 1)],
+        def store_scales(part, queues):
+            lines = slice(EARLY_TILES * P * part, EARLY_TILES * P * (part + 1))
+            for quad in range(P // 32):
+                queues[quad % len(queues)].dma_start(
+                    out=scale_rows(out_2[:, :, lines], quad), in_=quadrant(y_scales[part], quad)
                 )
-                if j % WORD_TILES == WORD_TILES - 1:
-                    first = P * (j + 1 - WORD_TILES)
+
+        def y_quantize(pair):
+            i, x = pair
+            for place, q in enumerate(groups[i][2 * x : 2 * x + 2]):
+                j, lh = divmod(q, HALVES)
+                words, at = y_words[j // WORD_TILES], P * (j % WORD_TILES)
+                part, line = j // EARLY_TILES, P * (j % EARLY_TILES)
+                quantize(
+                    words[:, lh, at : at + P], y_scales[part][:, lh, line : line + P],
+                    y_woven[pair][:, PASS * place : PASS * (place + 1)],
+                )
+                if (q + 1) % (HALVES * WORD_TILES) == 0:
+                    first = PACK * P * (j + 1 - WORD_TILES)
                     nc.sync.dma_start(
-                        out=out_1[lh].rearrange("p m t -> p (m t)")[:, PACK * first : PACK * P * (j + 1)].bitcast(I32),
+                        out=out_1.rearrange("g p m t -> p g (m t)")[:, :, first : PACK * P * (j + 1)].bitcast(I32),
                         in_=words[:].bitcast(I32),
                     )
-                if q == 2 * EARLY - 1:
+                if q == HALVES * EARLY_TILES - 1:
                     store_scales(0, [nc.sync])
-                if q == final:
+                if q == PIECES - 1:
                     store_scales(1, [nc.sync, nc.scalar])
 
-        def store_scales(part, queues):
-            m0, m1 = (0, EARLY * P) if part == 0 else (EARLY * P, N)
-            for q in range(4):
-                queues[q % len(queues)].dma_start(
-                    out=out_2[:, 4 * q : 4 * q + 4, m0:m1].rearrange("g r m -> r g m").bitcast(I32),
-                    in_=y_scales[part][32 * q : 32 * q + 4].bitcast(I32),
-                )
-
         def t_tile(j):
-            t_banks[j] = t_matmuls(j)
-            t_woven[j] = t_copy(t_banks[j])
+            t_matmuls(j)
+            t_copy(j)
 
-        a_weave_rest(2)
-        t_quantize(1, t_woven[1])
-        a_quantize(2)
+        finish_unit(2, 1)
         group_means(0)
-        for j in range(T_EARLY, 3):
-            t_tile(j)
-        ratios(4)
+        ratio_run(len(units))
         apply_guide(0)
-        a_weave_rest(3)
-        t_quantize(2, t_woven[2])
-        a_quantize(3)
+        finish_unit(3, 2)
         add_base(nc.vector, 0, 0, 1)
         add_base(nc.vector, 0, 1, 2)
-        t_tile(3)
+        store_y(0, 0)
+        t_tile(T_EARLY)
         group_means(1)
-        t_tile(4)
-        round_y(0, 0, 2)
-        turn_y((0, 0), (0, 2))
-        for i in (1, 2, 3):
-            apply_guide(i)
+        t_tile(T_EARLY + 1)
+        round_y("scalar", 0, 0, 2)
+        turn_y((0, 0))
+        for i in range(1, last):
             fresh = [j for j in (2 * i + 1, 2 * i + 2) if j < TILES]
-            t_quantize(fresh[0], t_woven[fresh[0]])
+            apply_guide(i)
+            t_quantize(fresh[0])
             add_base(nc.vector, i, 1, 2)
+            store_y(i, 0)
             add_base(nc.vector, i, 2, PACK)
+            store_y(i, 2)
             for j in fresh[1:]:
-                t_quantize(j, t_woven[j])
-            for pair in range(len(groups[i - 1]) // 2):
-                y_quantize((i - 1, pair))
+                t_quantize(j)
+            for x in range(len(groups[i - 1]) // 2):
+                y_quantize((i - 1, x))
             group_means(i + 1)
             for j in fresh:
                 if j + 2 < TILES:
                     t_tile(j + 2)
-            for pair in range(2):
-                round_y(i, 2 * pair, 2 * pair + 2)
-                turn_y((i, pair), (0, 2))
-        apply_guide(4)
-        add_base(nc.vector, 4, 0, 1)
-        add_base(nc.vector, 4, 1, 2)
-        round_y(4, 0, 1)
-        round_y(4, 1, 2)
-        turn_y((4, 0), (0, 2))
-        y_quantize((3, 0))
-        y_quantize((3, 1))
-        y_quantize((4, 0))
+            for x in range(2):
+                round_y("scalar", i, 2 * x, 2 * x + 2)
+                turn_y((i, x))
+        apply_guide(last)
+        for x in range(2):
+            add_base(nc.vector, last, x, x + 1)
+        store_y(last, 0)
+        for x in range(2):
+            round_y("vector", last, x, x + 1)
+        turn_y((last, 0))
+        for pair in ((last - 1, 0), (last - 1, 1), (last, 0)):
+            y_quantize(pair)

@@ -29,6 +29,7 @@ SCALE_ROWS = 4
 HEAD_SCALAR = 192
 A_GPSIMD = 192
 A_GPSIMD_LAST = 128
+A_SCALAR_LAST = 192
 BLEND_SCALAR_SLOT = 4
 T_SLOT = 10
 T_EARLY = 3
@@ -157,18 +158,19 @@ def tile_mean_free_guided_pass_k4_kernel(
             quantize(tiles[0][:], tiles[1][:], woven[:])
 
         def weave(engine, woven, rows, c0, c1):
+            run = 1 if engine == "gpsimd" else RUN
             copy_on(
                 engine,
-                woven[:, PACK * c0 : PACK * c1].rearrange("p (c j) -> p c j", j=PACK),
-                rows[:, :, c0:c1].rearrange("p j c -> p c j"),
+                woven[:, PACK * c0 : PACK * c1].rearrange("p (c i j) -> p c j i", i=run, j=PACK),
+                rows[:, :, c0:c1].rearrange("p j (c i) -> p c j i", i=run),
             )
 
         def weave_blend(engine, woven, g, h, t0, t1):
             rows = blend_rows[g][:, :, PASS * h : PASS * (h + 1)]
             copy_on(
                 engine,
-                woven[:].rearrange("p (t m r j) -> p t m r j", t=PACK, r=RUN, j=PACK)[:, t0:t1],
-                rows.rearrange("p j (m t r) -> p t m r j", t=PACK, r=RUN)[:, t0:t1],
+                woven[:].rearrange("p (t m r j) -> p m t j r", t=PACK, r=RUN, j=PACK)[:, :, t0:t1],
+                rows.rearrange("p j (m t r) -> p m t j r", t=PACK, r=RUN)[:, :, t0:t1],
             )
 
         def new_woven():
@@ -273,7 +275,11 @@ def tile_mean_free_guided_pass_k4_kernel(
                     weave("gpsimd", a_woven[u], a_rows[u], 0, gpsimd_share(u))
 
         def a_weave_rest(u):
-            weave("vector", a_woven[u], a_rows[u], gpsimd_share(u), PASS)
+            first = gpsimd_share(u)
+            if u == len(units) - 1:
+                weave("scalar", a_woven[u], a_rows[u], first, first + A_SCALAR_LAST)
+                first += A_SCALAR_LAST
+            weave("vector", a_woven[u], a_rows[u], first, PASS)
 
         def t_matmuls(j):
             t_sums[j] = [bank(T_BANKS, h) for h in halves]

from contextlib import ExitStack

import concourse.mybir as mybir
from concourse.masks import make_identity

N, L = 1024, 1024
FLOPS = 4 * 2 * N * N * L

F32 = mybir.dt.float32
BF16 = mybir.dt.bfloat16
I32 = mybir.dt.int32
U32 = mybir.dt.uint32
U8 = mybir.dt.uint8
FP8X4 = mybir.dt.float8_e4m3fn_x4
FP4X4 = mybir.dt.float4_e2m1fn_x4
ACT = mybir.ActivationFunctionType
ALU = mybir.AluOpType
ENG = mybir.EngineType

P = 128
PACK = 4
PASS = P * PACK
RUN = 4
HALVES = 2
TILES = N // P
PIECES = HALVES * TILES
SCALE_ROWS = 4

HEAD_SCALAR = 192
A_GPSIMD = 192
A_GPSIMD_LAST = 128
A_SCALAR_LAST = 192
BLEND_SCALAR_SLOT = 4
T_SLOT = 10
T_EARLY = 3

WORD_TILES = 2
EARLY_TILES = 4

DEN_BANKS, NUM_BANKS, T_BANKS = (0, 1), (2, 3, 4, 5), (6, 7)


def tile_mean_free_guided_pass_k4_kernel(
    tc, win_words, win_scales, cross_words, cross_scales, square, blend, conf, norm, guide, base,
    out_0, out_1, out_2,
):
    nc = tc.nc
    with ExitStack() as ctx:
        keep = ctx.enter_context(tc.tile_pool(name="keep", bufs=1))
        work = ctx.enter_context(tc.tile_pool(name="work", bufs=2))
        psum = ctx.enter_context(tc.psum_pool(name="psum", bufs=1))
        ctx.enter_context(tc.manual_schedule(engines={ENG.SP, ENG.DVE, ENG.Pool}))

        def kept(name, shape, dtype):
            return keep.tile(shape, dtype, name=name, align_bytes=64)

        def rotating(tag, shape, dtype, bufs):
            return work.tile(shape, dtype, name=tag, tag=tag, bufs=bufs, align_bytes=64)

        def bank(banks, count):
            name = "bank%d" % banks[count % len(banks)]
            return psum.tile([P, PASS], F32, name=name, tag=name)

        def quantised(name, key, width):
            return kept("%s_codes%s" % (name, key), [P, width], U32), kept("%s_scales%s" % (name, key), [P, width], U8)

        halves = range(HALVES)
        pairs = [(a, b) for a in halves for b in halves]
        v_words = [kept("v_words%d" % h, [P, HALVES, N], U8) for h in halves]
        v_scales = kept("v_scales", [P, HALVES, N], U8)
        v_words_sorted = [kept("v_words_sorted%d" % h, [P, HALVES, N], U8) for h in halves]
        v_scales_sorted = kept("v_scales_sorted", [P, HALVES, N], U8)
        c_scales = kept("c_scales", [P, HALVES, L], U8)
        c_words = [kept("c_words%d" % lh, [P, HALVES, PASS], U32) for lh in halves]
        square_rows = {(g, lh): kept("square_rows%d%d" % (g, lh), [P, PACK, PASS], BF16) for g, lh in pairs}
        blend_rows = [kept("blend_rows%d" % g, [P, PACK, N], BF16) for g in halves]
        guide_sb = kept("guide_sb", [P, TILES * L], BF16)
        base_sb = kept("base_sb", [P, TILES * L], BF16)
        square_q = {(g, lh): quantised("square", "%d%d" % (g, lh), PASS) for g, lh in pairs}
        blend_q = {(g, h): quantised("blend", "%d%d" % (g, h), PASS) for g, h in pairs}
        a_q = {(h, lh): quantised("a", "%d%d" % (h, lh), PASS) for h, lh in pairs}
        t_q = [quantised("t", "%d" % j, HALVES * P) for j in range(TILES)]
        y_words = [kept("y_words%d" % i, [P, HALVES, WORD_TILES * P], U32) for i in range(TILES // WORD_TILES)]
        y_scales = [kept("y_scales%d" % part, [P, HALVES, EARLY_TILES * P], U8) for part in range(TILES // EARLY_TILES)]
        line_rows = kept("line_rows", [P, PASS + P], BF16)
        conf_sorted = kept("conf_sorted", [P, PASS], BF16)
        identity = kept("identity", [P, P], F32)
        identity_bf = kept("identity_bf", [P, TILES], BF16)
        line_cols = kept("line_cols", [P, 2 * TILES], F32)

        nc.gpsimd.memset(line_rows[:], 0.0)
        nc.scalar.dma_start(out=line_rows[0:HALVES, 0:PASS], in_=conf.rearrange("(h c) -> h c", h=HALVES))
        nc.scalar.dma_start(out=line_rows[0:TILES, PASS:], in_=norm.rearrange("(j p) -> j p", p=P))
        make_identity(nc, identity[:])
        nc.gpsimd.tensor_copy(out=identity_bf[:], in_=identity[:, 0:TILES])
        nc.vector.memset(v_scales[:].rearrange("p g n -> p (g n)").bitcast(I32), 0)
        nc.vector.memset(c_scales[:].rearrange("p g n -> p (g n)").bitcast(I32), 0)

        def quadrant(plane, quad):
            return plane[32 * quad : 32 * quad + SCALE_ROWS].bitcast(I32)

        def scale_rows(dram, quad):
            return dram[:, SCALE_ROWS * quad : SCALE_ROWS * (quad + 1), :].rearrange("g r n -> r g n").bitcast(I32)

        def load_scales(plane, dram):
            for quad in range(P // 32):
                nc.sync.dma_start(out=quadrant(plane, quad), in_=scale_rows(dram, quad))

        def by_word(rows):
            return rows.rearrange("(p j) x -> p j x", j=PACK)

        def load_square(g, lh):
            rows = square[PASS * g : PASS * (g + 1), PASS * lh : PASS * (lh + 1)]
            nc.sync.dma_start(out=square_rows[g, lh][:], in_=by_word(rows))

        def load_blend(g):
            nc.sync.dma_start(out=blend_rows[g][:], in_=by_word(blend[PASS * g : PASS * (g + 1), :]))

        def load_window(h):
            columns = win_words.rearrange("g p b -> p g b")[:, :, N * h : N * (h + 1)]
            nc.sync.dma_start(out=v_words[h][:].bitcast(I32), in_=columns.bitcast(I32))

        def load_cross(lh):
            columns = cross_words.rearrange("g p l t -> p g (l t)")[:, :, PACK * PASS * lh : PACK * PASS * (lh + 1)]
            nc.sync.dma_start(out=c_words[lh][:].bitcast(I32), in_=columns.bitcast(I32))

        load_square(0, 0)
        load_square(1, 0)
        load_window(0)
        load_scales(v_scales, win_scales)
        load_square(0, 1)
        load_scales(c_scales, cross_scales)
        load_cross(0)
        load_window(1)
        load_square(1, 1)
        load_blend(1)
        load_blend(0)
        load_cross(1)
        for i in range(TILES // 2):
            for tile_sb, dram in ((guide_sb, guide), (base_sb, base)):
                nc.sync.dma_start(
                    out=tile_sb[:, 2 * L * i : 2 * L * (i + 1)].rearrange("p (j l) -> p j l", j=2),
                    in_=dram[2 * P * i : 2 * P * (i + 1), :].rearrange("(j p) l -> p j l", p=P),
                )

        def copy_on(engine, out, in_):
            if engine == "scalar":
                nc.scalar.copy(out=out, in_=in_)
            elif engine == "gpsimd":
                nc.gpsimd.tensor_scalar(out=out, in0=in_, scalar1=1.0, scalar2=1.0, op0=ALU.mult, op1=ALU.mult)
            else:
                nc.vector.tensor_copy(out=out, in_=in_)

        def quantize(codes, scales, woven):
            nc.vector.quantize_mx(out=codes.bitcast(FP8X4), scales=scales, in_=woven)

        def quantize_tile(tiles, woven):
            quantize(tiles[0][:], tiles[1][:], woven[:])

        def weave(engine, woven, rows, c0, c1):
            run = 1 if engine == "gpsimd" else RUN
            copy_on(
                engine,
                woven[:, PACK * c0 : PACK * c1].rearrange("p (c i j) -> p c j i", i=run, j=PACK),
                rows[:, :, c0:c1].rearrange("p j (c i) -> p c j i", i=run),
            )

        def weave_blend(engine, woven, g, h, t0, t1):
            rows = blend_rows[g][:, :, PASS * h : PASS * (h + 1)]
            copy_on(
                engine,
                woven[:].rearrange("p (t m r j) -> p m t j r", t=PACK, r=RUN, j=PACK)[:, :, t0:t1],
                rows.rearrange("p j (m t r) -> p m t j r", t=PACK, r=RUN)[:, :, t0:t1],
            )

        def new_woven():
            return rotating("woven", [P, PACK * PASS], BF16, 5)

        def woven_square(g, lh):
            woven = new_woven()
            weave("vector", woven, square_rows[g, lh], 0, PASS)
            return woven

        def woven_blend(g, h):
            woven = new_woven()
            weave_blend("vector", woven, g, h, 0, PACK)
            return woven

        def sort_window(h):
            nc.vector.tensor_copy(
                out=v_words_sorted[h][:].bitcast(I32).rearrange("p g (t m w) -> p g t m w", t=PACK, w=2),
                in_=v_words[h][:].bitcast(I32).rearrange("p g (m t w) -> p g t m w", t=PACK, w=2),
            )

        def sort_window_scales():
            nc.vector.tensor_copy(
                out=v_scales_sorted[:].bitcast(I32).rearrange("p g (h t m) -> p (g h) t m", h=HALVES, t=PACK),
                in_=v_scales[:].bitcast(I32).rearrange("p g (h m t) -> p (g h) t m", h=HALVES, t=PACK),
            )

        head = [new_woven() for g in halves]
        weave("scalar", head[0], square_rows[0, 0], 0, HEAD_SCALAR)
        weave("vector", head[0], square_rows[0, 0], HEAD_SCALAR, PASS)
        sort_window_scales()
        quantize_tile(square_q[0, 0], head[0])
        weave("scalar", head[1], square_rows[1, 0], 0, HEAD_SCALAR)
        weave("vector", head[1], square_rows[1, 0], HEAD_SCALAR, PASS)
        sort_window(0)
        quantize_tile(square_q[1, 0], head[1])

        def line_columns():
            nc.scalar.copy(
                out=conf_sorted[:].rearrange("h (t m r) -> h t m r", t=PACK, r=RUN),
                in_=line_rows[:, 0:PASS].rearrange("h (m t r) -> h t m r", t=PACK, r=RUN),
            )
            turned_lines = bank(T_BANKS, 1)
            blocks = [(conf_sorted[:, P * t : P * (t + 1)], HALVES * t, HALVES) for t in range(PACK)]
            for rows, first, count in blocks + [(line_rows[:, PASS:], TILES, TILES)]:
                nc.tensor.matmul(
                    turned_lines[:, first : first + count], lhsT=rows, rhs=identity_bf[:, 0:count], start=True, stop=True
                )
            nc.scalar.copy(out=line_cols[:], in_=turned_lines[:, 0 : 2 * TILES])

        units = [(h, lh) for lh in halves for h in halves]
        slots = len(units) * PACK
        root, recip, nums, a_rows, a_woven, t_sums, t_woven = {}, {}, {}, {}, {}, {}, {}

        def moment(s, operand, banks):
            (h, lh), t = units[s // PACK], s % PACK
            acc = bank(banks, s)
            for g in halves:
                codes, scales = operand(g, lh)
                nc.tensor.matmul_mx(
                    out=acc[:],
                    lhsT=v_words_sorted[h][:, g, 2 * P * t : 2 * P * (t + 1)].bitcast(FP4X4),
                    lhsT_scale=v_scales_sorted[:, g, PASS * h + P * t : PASS * h + P * (t + 1)],
                    rhs=codes.bitcast(FP8X4), rhs_scale=scales,
                    start=(g == 0), stop=(g == HALVES - 1),
                )
            return acc

        def square_operand(g, lh):
            return square_q[g, lh][0][:], square_q[g, lh][1][:]

        def cross_operand(g, lh):
            return c_words[lh][:, g, :], c_scales[:, g, PASS * lh : PASS * (lh + 1)]

        def inverse_root(s, den):
            root[s] = rotating("root", [P, PASS], F32, 2)
            nc.scalar.activation(out=root[s][:], in_=den[:], func=ACT.Abs_reciprocal_sqrt)

        def reciprocal(s):
            recip[s] = rotating("recip", [P, PASS], F32, PACK + 1)
            nc.scalar.activation(out=recip[s][:], in_=root[s][:], func=ACT.Square)

        def ratio(s):
            u, t = divmod(s, PACK)
            if t == 0:
                a_rows[u] = rotating("a_rows", [P, PACK, PASS], BF16, 2)
            column = HALVES * t + units[u][0]
            nc.vector.scalar_tensor_tensor(
                out=a_rows[u][:, t, :], in0=nums[s][:], scalar=line_cols[:, column : column + 1], in1=recip[s][:],
                op0=ALU.mult, op1=ALU.mult,
            )

        def gpsimd_share(u):
            return A_GPSIMD_LAST if u == len(units) - 1 else A_GPSIMD

        def ratio_run(b):
            for s in range(max(PACK * b - 1, 0), min(PACK * (b + 1) - 1, slots)):
                ratio(s)
                if s % PACK == PACK - 1:
                    u = s // PACK
                    a_woven[u] = rotating("a_woven", [P, PACK * PASS], BF16, 2)
                    weave("gpsimd", a_woven[u], a_rows[u], 0, gpsimd_share(u))

        def a_weave_rest(u):
            first = gpsimd_share(u)
            if u == len(units) - 1:
                weave("scalar", a_woven[u], a_rows[u], first, first + A_SCALAR_LAST)
                first += A_SCALAR_LAST
            weave("vector", a_woven[u], a_rows[u], first, PASS)

        def t_matmuls(j):
            t_sums[j] = [bank(T_BANKS, h) for h in halves]
            window = v_words[j // PACK]
            for h in halves:
                for t in range(PACK):
                    for g in halves:
                        nc.tensor.matmul_mx(
                            out=t_sums[j][h][:, P * t : P * (t + 1)],
                            lhsT=blend_q[g, h][0][:, P * t : P * (t + 1)].bitcast(FP8X4),
                            lhsT_scale=blend_q[g, h][1][:, P * t : P * (t + 1)],
                            rhs=window[:, g, 2 * P * (j % PACK) : 2 * P * (j % PACK + 1)].bitcast(FP4X4),
                            rhs_scale=v_scales[:, g, P * j : P * (j + 1)],
                            start=(g == 0), stop=(g == HALVES - 1),
                        )

        def t_copy(j):
            t_woven[j] = rotating("t_woven", [P, HALVES * PASS], BF16, T_EARLY)
            for h in halves:
                nc.scalar.copy(
                    out=t_woven[j][:, PASS * h : PASS * (h + 1)].rearrange("p (n t) -> p n t", t=PACK),
                    in_=t_sums[j][h][:].rearrange("p (t n) -> p n t", t=PACK),
                )

        def t_quantize(j):
            quantize_tile(t_q[j], t_woven[j])

        def finish_unit(u, j):
            a_weave_rest(u)
            t_quantize(j)
            quantize_tile(a_q[units[u]], a_woven[u])

        def before_run_0():
            woven = woven_square(0, 1)
            sort_window(1)
            quantize_tile(square_q[0, 1], woven)

        def before_run_1():
            last_square = woven_square(1, 1)
            first_blend = woven_blend(1, 0)
            quantize_tile(square_q[1, 1], last_square)
            second_blend = woven_blend(1, 1)
            quantize_tile(blend_q[1, 0], first_blend)
            quantize_tile(blend_q[1, 1], second_blend)

        def before_run_2(last_blend):
            third_blend = woven_blend(0, 0)
            a_weave_rest(0)
            quantize_tile(blend_q[0, 0], third_blend)
            quantize_tile(blend_q[0, 1], last_blend)
            quantize_tile(a_q[units[0]], a_woven[0])

        line_columns()
        before_run_0()
        for s in range(slots):
            b, t = divmod(s, PACK)
            den = moment(s, square_operand, DEN_BANKS)
            if t < PACK - 1:
                nums[s] = moment(s, cross_operand, NUM_BANKS)
            inverse_root(s, den)
            if s > 0:
                reciprocal(s - 1)
            if s == BLEND_SCALAR_SLOT:
                scalar_blend = new_woven()
            if 0 <= s - BLEND_SCALAR_SLOT < PACK:
                weave_blend("scalar", scalar_blend, 0, 1, s - BLEND_SCALAR_SLOT, s - BLEND_SCALAR_SLOT + 1)
            j, second = divmod(s - T_SLOT, 2)
            if 0 <= j < T_EARLY:
                (t_copy if second else t_matmuls)(j)
            if t == PACK - 1:
                if b == len(units) - 1:
                    finish_unit(1, 0)
                ratio_run(b)
                nums[s] = moment(s, cross_operand, NUM_BANKS)
                if b == 0:
                    before_run_1()
                if b == 1:
                    before_run_2(scalar_blend)
        reciprocal(slots - 1)

        first_group, last_group = [0, 2], [PIECES - 2, PIECES - 1]
        middle = [q for q in range(PIECES) if q not in first_group + last_group]
        groups = [first_group] + [middle[x : x + PACK] for x in range(0, len(middle), PACK)] + [last_group]
        last = len(groups) - 1
        means, ys, y_bf, y_woven = {}, {}, {}, {}

        def parts(q, width):
            return [(0, width // 2), (width // 2, width)] if q == PIECES - 1 else [(0, width)]

        def group_means(i):
            for q in groups[i]:
                j, lh = divmod(q, HALVES)
                means[q] = bank(NUM_BANKS, len(means))
                for h in halves:
                    nc.tensor.matmul_mx(
                        out=means[q][:],
                        lhsT=t_q[j][0][:, P * h : P * (h + 1)].bitcast(FP8X4),
                        lhsT_scale=t_q[j][1][:, P * h : P * (h + 1)],
                        rhs=a_q[h, lh][0][:].bitcast(FP8X4), rhs_scale=a_q[h, lh][1][:],
                        start=(h == 0), stop=(h == HALVES - 1),
                    )

        def apply_guide(i):
            ys[i] = rotating("y", [P, PACK * PASS], F32, 3)
            for x, q in enumerate(groups[i]):
                column = TILES + q // HALVES
                for c0, c1 in parts(q, PASS):
                    nc.vector.scalar_tensor_tensor(
                        out=ys[i][:, PASS * x + c0 : PASS * x + c1], in0=means[q][:, c0:c1],
                        scalar=line_cols[:, column : column + 1],
                        in1=guide_sb[:, PASS * q + c0 : PASS * q + c1], op0=ALU.mult, op1=ALU.mult,
                    )
                if x == 0 and len(groups[i]) == PACK:
                    add_base(nc.gpsimd, i, 0, 1)

        def add_base(engine, i, x0, x1):
            first = PASS * groups[i][x0]
            for c0, c1 in parts(groups[i][x0], PASS * (x1 - x0)):
                part = ys[i][:, PASS * x0 + c0 : PASS * x0 + c1]
                engine.tensor_tensor(out=part, in0=part, in1=base_sb[:, first + c0 : first + c1], op=ALU.add)

        def store_y(i, x):
            tiles = [groups[i][x] // HALVES, groups[i][x + 1] // HALVES]
            if tiles[0] == tiles[1]:
                nc.sync.dma_start(out=out_0[P * tiles[0] : P * (tiles[0] + 1), :], in_=ys[i][:, PASS * x : PASS * (x + 2)])
                return
            for place, j in enumerate(tiles, start=x):
                lh = groups[i][place] % HALVES
                nc.sync.dma_start(
                    out=out_0[P * j : P * (j + 1), PASS * lh : PASS * (lh + 1)],
                    in_=ys[i][:, PASS * place : PASS * (place + 1)],
                )

        def round_y(engine, i, x0, x1):
            pair = (i, x0 // 2)
            if x0 % 2 == 0:
                y_bf[pair] = rotating("y_bf", [P, 2 * PASS], BF16, 3)
            rounded = y_bf[pair][:, PASS * (x0 % 2) : PASS * (x0 % 2 + x1 - x0)]
            for p0, p1 in parts(groups[i][x0], P):
                copy_on(
                    engine,
                    rounded.rearrange("n (x u p e) -> n x u p e", u=2, p=P, e=2)[:, :, :, p0:p1],
                    ys[i][:, PASS * x0 : PASS * x1].rearrange("n (x p u e) -> n x u p e", u=2, p=P, e=2)[:, :, :, p0:p1],
                )

        def turn_y(pair):
            turned = bank(DEN_BANKS, len(y_woven))
            words = y_bf[pair][:].bitcast(F32)
            for block in range(PASS // P):
                nc.tensor.transpose(
                    turned[:, P * block : P * (block + 1)], words[:, P * block : P * (block + 1)], identity[:]
                )
            y_woven[pair] = rotating("y_woven", [P, 2 * PASS], BF16, 3)
            nc.scalar.copy(
                out=y_woven[pair][:].bitcast(F32).rearrange("p (x n u) -> p x n u", n=P, u=2),
                in_=turned[:].rearrange("p (x u n) -> p x n u", n=P, u=2),
            )

        def store_scales(part, queues):
            lines = slice(EARLY_TILES * P * part, EARLY_TILES * P * (part + 1))
            for quad in range(P // 32):
                queues[quad % len(queues)].dma_start(
                    out=scale_rows(out_2[:, :, lines], quad), in_=quadrant(y_scales[part], quad)
                )

        def y_quantize(pair):
            i, x = pair
            for place, q in enumerate(groups[i][2 * x : 2 * x + 2]):
                j, lh = divmod(q, HALVES)
                words, at = y_words[j // WORD_TILES], P * (j % WORD_TILES)
                part, line = j // EARLY_TILES, P * (j % EARLY_TILES)
                quantize(
                    words[:, lh, at : at + P], y_scales[part][:, lh, line : line + P],
                    y_woven[pair][:, PASS * place : PASS * (place + 1)],
                )
                if (q + 1) % (HALVES * WORD_TILES) == 0:
                    first = PACK * P * (j + 1 - WORD_TILES)
                    nc.sync.dma_start(
                        out=out_1.rearrange("g p m t -> p g (m t)")[:, :, first : PACK * P * (j + 1)].bitcast(I32),
                        in_=words[:].bitcast(I32),
                    )
                if q == HALVES * EARLY_TILES - 1:
                    store_scales(0, [nc.sync])
                if q == PIECES - 1:
                    store_scales(1, [nc.sync, nc.scalar])

        def t_tile(j):
            t_matmuls(j)
            t_copy(j)

        finish_unit(2, 1)
        group_means(0)
        ratio_run(len(units))
        apply_guide(0)
        finish_unit(3, 2)
        add_base(nc.vector, 0, 0, 1)
        add_base(nc.vector, 0, 1, 2)
        store_y(0, 0)
        t_tile(T_EARLY)
        group_means(1)
        t_tile(T_EARLY + 1)
        round_y("scalar", 0, 0, 2)
        turn_y((0, 0))
        for i in range(1, last):
            fresh = [j for j in (2 * i + 1, 2 * i + 2) if j < TILES]
            apply_guide(i)
            t_quantize(fresh[0])
            add_base(nc.vector, i, 1, 2)
            store_y(i, 0)
            add_base(nc.vector, i, 2, PACK)
            store_y(i, 2)
            for j in fresh[1:]:
                t_quantize(j)
            for x in range(len(groups[i - 1]) // 2):
                y_quantize((i - 1, x))
            group_means(i + 1)
            for j in fresh:
                if j + 2 < TILES:
                    t_tile(j + 2)
            for x in range(2):
                round_y("scalar", i, 2 * x, 2 * x + 2)
                turn_y((i, x))
        apply_guide(last)
        for x in range(2):
            add_base(nc.vector, last, x, x + 1)
        store_y(last, 0)
        for x in range(2):
            round_y("vector", last, x, x + 1)
        turn_y((last, 0))
        for pair in ((last - 1, 0), (last - 1, 1), (last, 0)):
            y_quantize(pair)
